import numpy as np
import ml_dtypes


def mxq(x, axis, fmt="e4m3"):
    dtype, down = {"e4m3": (ml_dtypes.float8_e4m3fn, 7), "e5m2": (ml_dtypes.float8_e5m2, 14)}[fmt]
    v = np.moveaxis(np.asarray(x, np.float32).astype(ml_dtypes.bfloat16).astype(np.float64), axis, -1)
    blocks = v.reshape(v.shape[:-1] + (-1, 32))
    amax = np.abs(blocks).max(-1, keepdims=True)
    byte = np.maximum(np.where(amax > 0, np.frexp(amax)[1] - 1 + 127, 0) - down, 1)
    scale = np.exp2(byte - 127.0)
    codes = (blocks / scale).astype(np.float32).astype(dtype).astype(np.float64)
    return np.moveaxis((codes * scale).reshape(v.shape), -1, axis)


WIDE = False


def mx_kscale(k):
    if not WIDE:
        return np.ones(k)
    levels = np.array([10, -10, 5, -5, 0])
    if k % 512:
        return np.exp2(np.random.permutation(np.resize(levels, k // 32))).repeat(32)
    a = np.empty((k // 512, 16))
    for p in range(k // 512):
        a[p, :8] = np.random.permutation(np.resize(levels, 8))
        for g in range(8):
            far = levels[np.abs(levels - a[p, g]) >= 10]
            a[p, g + 8] = far[np.random.randint(len(far))]
    return np.exp2(a.ravel()).repeat(32)


def f64(x):
    return np.asarray(x).astype(np.float64)


def striped(idx):
    return np.tile(np.asarray(idx).reshape(-1, 16).T, (8, 1)).astype(np.uint16)


def unstriped(offs):
    return offs[:16].T.reshape(-1).astype(np.int64)


E2M1 = np.array([0.0, 0.5, 1.0, 1.5, 2.0, 3.0, 4.0, 6.0, -0.0, -0.5, -1.0, -1.5, -2.0, -3.0, -4.0, -6.0])


def pack_weight(w, fmt):
    k, n = w.shape
    w = f64(np.asarray(w, np.float32).astype(ml_dtypes.bfloat16)).reshape(k // 32, 32, n)
    amax = np.abs(w).max(1)
    if fmt == "e4m3":
        byte = np.frexp(amax)[1] - 1 + 127 - 7
    else:
        mant, ex = np.frexp(amax / 6.0)
        byte = np.where(mant > 0.5, ex, ex - 1) + 127
    byte = np.clip(np.where(amax > 0, byte, 1), 1, 254)
    scaled = (w * np.exp2(127.0 - byte)[:, None, :]).reshape(k, n).astype(np.float32)
    by_word = np.ascontiguousarray(scaled.reshape(k // 512, 128, 4, n).transpose(0, 1, 3, 2))
    if fmt == "e4m3":
        words = by_word.astype(ml_dtypes.float8_e4m3fn).view(np.uint8)
    else:
        c = by_word.astype(ml_dtypes.float4_e2m1fn).view(np.uint8) & 0xF
        words = (c[..., 0::2] | (c[..., 1::2] << 4)).reshape(k // 512, 128, 2 * n)
    return np.ascontiguousarray(words), np.ascontiguousarray(byte.astype(np.uint8).reshape(k // 512, 16, n))


def unpack_weight(words, scales, fmt):
    g, _, n = scales.shape
    words = np.ascontiguousarray(words).reshape(g, 128, n, -1)
    if fmt == "e4m3":
        vals = words.view(ml_dtypes.float8_e4m3fn).astype(np.float64)
    else:
        nib = np.empty((g, 128, n, 4), np.uint8)
        nib[..., 0::2] = words & 0xF
        nib[..., 1::2] = words >> 4
        vals = E2M1[nib]
    vals = vals * np.repeat(np.exp2(scales.astype(np.float64) - 127.0), 8, axis=1)[..., None]
    return vals.transpose(0, 1, 3, 2).reshape(g * 512, n)


def rot(x):
    y = x.reshape(-1, 2, x.shape[1])
    return np.stack([-y[:, 1], y[:, 0]], axis=1).reshape(x.shape)


def bf(x):
    return np.asarray(x, np.float32).astype(ml_dtypes.bfloat16)


def planes(Y):
    r, m = Y.shape
    b = f64(bf(Y)).reshape(r // 32, 32, m)
    amax = np.abs(b).max(1)
    byte = np.clip(np.where(amax > 0, np.frexp(amax)[1] - 1 + 127 - 7, 1), 1, 254)
    codes = (b * np.exp2(127.0 - byte)[:, None, :]).reshape(r, m).astype(np.float32).astype(ml_dtypes.float8_e4m3fn).view(np.uint8)
    words = codes.reshape(r // 512, 128, 4, m).transpose(0, 1, 3, 2)
    return np.ascontiguousarray(words), np.ascontiguousarray(byte.astype(np.uint8).reshape(r // 512, 16, m))


K, T, I, D, U = 512, 2048, 512, 512, 1024


def setup_inputs():
    n = np.random.standard_normal
    idx = np.random.permutation(T)[:I]
    idx2 = np.random.randint(0, U, I)
    fk = mx_kscale(K)
    embp = pack_weight(n((K, T)) / fk[:, None], "e4m3")
    return {
        "emb_words": embp[0],
        "emb_scales": embp[1],
        "wk": (n((K, D)) * 1 / np.sqrt(K) * fk[:, None]).astype(np.float32),
        "cosn": (np.repeat(np.round(np.cos(np.arange(D // 2)[:, None] * 0.11 + np.arange(U)[None] * 0.37) * 64) / 64, 2, axis=0)).astype(np.float32),
        "sinn": (np.repeat(np.round(np.sin(np.arange(D // 2)[:, None] * 0.11 + np.arange(U)[None] * 0.37) * 64) / 64, 2, axis=0)).astype(np.float32),
        "offs": striped(idx),
        "offs2": striped(idx2),
    }


def reference(emb_words, emb_scales, wk, cosn, sinn, offs, offs2):
    idx = unstriped(offs)
    idx2 = unstriped(offs2)
    embu = unpack_weight(emb_words, emb_scales, "e4m3")
    wkq = mxq(f64(wk), 0, "e4m3")
    embidxg = embu[:, idx]
    b = wkq.T @ embidxg
    br = rot(b)
    y = b * f64(cosn)[:, idx2] + br * f64(sinn)[:, idx2]
    words, scales = planes(y)
    return y, words, scales

@@ -1,0 +1,109 @@
+from contextlib import ExitStack
+
+import concourse.mybir as mybir
+
+K, T, I, D, U = 512, 2048, 512, 512, 1024
+FLOPS = 2 * K * D * I
+BYTES = 128 * T * 4 + 16 * T + K * D * 4 + 2 * (D // 2) * U * 4 + 2 * 128 * 32 * 2 + D * I * 4 + D * I + 16 * I
+
+F32 = mybir.dt.float32
+BF16 = mybir.dt.bfloat16
+I32 = mybir.dt.int32
+U32 = mybir.dt.uint32
+U16 = mybir.dt.uint16
+U8 = mybir.dt.uint8
+FP8X4 = mybir.dt.float8_e4m3fn_x4
+MULT = mybir.AluOpType.mult
+ADD = mybir.AluOpType.add
+SUB = mybir.AluOpType.subtract
+
+P = 128
+PACK = 4
+CH = 128
+NCH = I // CH
+
+
+def tile_attend_freshrope_pl_kernel(tc, emb_words, emb_scales, wk, cosn, sinn, offs, offs2, out_0, out_1, out_2):
+    nc = tc.nc
+    with ExitStack() as ctx:
+        sb = ctx.enter_context(tc.tile_pool(name="sb", bufs=1))
+        ps = ctx.enter_context(tc.psum_pool(name="ps", bufs=1))
+
+        tok = sb.tile([P, I // 16], U16, name="tok")
+        pos = sb.tile([P, I // 16], U16, name="pos")
+        w_raw = sb.tile([P, PACK, D], F32, name="w_raw")
+        e_pool = sb.tile([P, T], I32, name="e_pool", align_bytes=64)
+        s_pool = sb.tile([P, T], U8, name="s_pool", align_bytes=64)
+        tabs = [[sb.tile([P, U], F32, name="tab%d%d" % (n, a)) for a in range(2)] for n in range(2)]
+
+        nc.vector.memset(s_pool[:].bitcast(I32), 0)
+        nc.sync.dma_start(w_raw[:], wk.rearrange("(p j) d -> p j d", j=PACK))
+        nc.sync.dma_start(tok[:], offs)
+        for q in range(4):
+            nc.sync.dma_start(s_pool[32 * q : 32 * q + 4, :].bitcast(I32), emb_scales[0, 4 * q : 4 * q + 4, :].bitcast(I32))
+        nc.sync.dma_start(e_pool[:], emb_words[0].rearrange("p n t -> p (n t)").bitcast(I32))
+        nc.sync.dma_start(pos[:], offs2)
+        for a in range(2):
+            for n, src in enumerate((cosn, sinn)):
+                nc.sync.dma_start(tabs[n][a][:], src.rearrange("(p t) u -> p t u", t=PACK)[:, 2 * a, :])
+
+        e_scales = sb.tile([P, I], U8, name="e_scales", align_bytes=64)
+        nc.vector.tensor_copy(e_scales[:], s_pool[:].indirect(tok[:]))
+
+        w_codes = sb.tile([P, D], U32, name="w_codes", align_bytes=64)
+        w_scales = sb.tile([P, D], U8, name="w_scales", align_bytes=64)
+        w_view = w_raw[:].rearrange("p j (m t) -> p m t j", t=PACK)
+        for h in range(2):
+            w_bf = sb.tile([P, 2, P, PACK], BF16, name="w_bf%d" % h, align_bytes=64)
+            dst = w_bf[:].rearrange("p t m j -> p m t j")
+            if h == 0:
+                nc.vector.tensor_copy(dst, w_view[:, :, 0:2, :])
+            else:
+                nc.scalar.copy(dst, w_view[:, :, 2:4, :])
+            cols = slice(2 * P * h, 2 * P * (h + 1))
+            nc.vector.quantize_mx(out=w_codes[:, cols].bitcast(FP8X4), scales=w_scales[:, cols], in_=w_bf[:].rearrange("p t m j -> p (t m j)"))
+
+        e_codes = sb.tile([P, I], U32, name="e_codes", align_bytes=64)
+        nc.vector.tensor_copy(e_codes[:], e_pool[:].bitcast(U32).indirect(tok[:]))
+
+        banks = []
+        for c in range(NCH):
+            bank = ps.tile([P, PACK, CH], F32, name="bank%d" % c)
+            cols = slice(c * CH, (c + 1) * CH)
+            for t in range(PACK):
+                wc = slice(t * P, (t + 1) * P)
+                nc.tensor.matmul_mx(out=bank[:, t, :], lhsT=w_codes[:, wc].bitcast(FP8X4), lhsT_scale=w_scales[:, wc],
+                                    rhs=e_codes[:, cols].bitcast(FP8X4), rhs_scale=e_scales[:, cols], start=True, stop=True)
+            banks.append(bank)
+
+        trig = [sb.tile([P, 2, I], F32, name="trig%d" % n) for n in range(2)]
+        for a in range(2):
+            for n in range(2):
+                nc.vector.tensor_copy(trig[n][:, a, :], tabs[n][a][:].indirect(pos[:]))
+
+        y_bf = sb.tile([P, I, PACK], BF16, name="y_bf", align_bytes=64)
+        y_codes = sb.tile([P, I], U32, name="y_codes", align_bytes=64)
+        y_scales = sb.tile([P, I], U8, name="y_scales", align_bytes=64)
+        out_view = out_0.rearrange("(p t) i -> p t i", t=PACK)
+        for c in range(NCH):
+            cols = slice(c * CH, (c + 1) * CH)
+            prods = []
+            for n in range(2):
+                prod = sb.tile([P, 2, 2, CH], F32, name="prod%d%d" % (c, n))
+                nc.vector.tensor_tensor(prod[:], banks[c][:].rearrange("p (a e) i -> p a e i", e=2),
+                                        trig[n][:, :, cols].unsqueeze(2).to_broadcast([P, 2, 2, CH]), MULT)
+                prods.append(prod)
+            y = sb.tile([P, 2, 2, CH], F32, name="y%d" % c)
+            eng = nc.vector if c == NCH - 1 else nc.gpsimd
+            eng.tensor_tensor(y[:, :, 0, :], prods[0][:, :, 0, :], prods[1][:, :, 1, :], SUB)
+            eng.tensor_tensor(y[:, :, 1, :], prods[0][:, :, 1, :], prods[1][:, :, 0, :], ADD)
+            nc.sync.dma_start(out_view[:, :, cols], y[:].rearrange("p a e i -> p (a e) i"))
+            nc.scalar.copy(y_bf[:, cols, :].rearrange("p (g i) t -> p g t i", i=4), y[:].rearrange("p a e (g i) -> p g (a e) i", i=4))
+
+        words = out_1[0].rearrange("p n t -> p (n t)").bitcast(I32)
+        for lo, hi in ((0, 256), (256, 384), (384, 512)):
+            nc.vector.quantize_mx(out=y_codes[:, lo:hi].bitcast(FP8X4), scales=y_scales[:, lo:hi], in_=y_bf[:, lo:hi, :].rearrange("p i t -> p (i t)"))
+        for lo, hi in ((0, 256), (256, 512)):
+            nc.sync.dma_start(words[:, lo:hi], y_codes[:, lo:hi].bitcast(I32))
+        for q in range(4):
+            nc.scalar.dma_start(out_2[0, 4 * q : 4 * q + 4, :].bitcast(I32), y_scales[32 * q : 32 * q + 4, :].bitcast(I32))

@@ -21,6 +21,7 @@ P = 128
 PACK = 4
 CH = 128
 NCH = I // CH
+NG = 3
 
 
 def tile_attend_freshrope_pl_kernel(tc, emb_words, emb_scales, wk, cosn, sinn, offs, offs2, out_0, out_1, out_2):
@@ -34,32 +35,39 @@ def tile_attend_freshrope_pl_kernel(tc, emb_words, emb_scales, wk, cosn, sinn, o
         w_raw = sb.tile([P, PACK, D], F32, name="w_raw")
         e_pool = sb.tile([P, T], I32, name="e_pool", align_bytes=64)
         s_pool = sb.tile([P, T], U8, name="s_pool", align_bytes=64)
-        tabs = [[sb.tile([P, U], F32, name="tab%d%d" % (n, a)) for a in range(2)] for n in range(2)]
+        tabs = [[sb.tile([P, U], F32, name="tab%d%d" % (n, a), tag="tab%d%d" % (n, a)) for a in range(2)] for n in range(2)]
 
         nc.vector.memset(s_pool[:].bitcast(I32), 0)
-        nc.sync.dma_start(w_raw[:], wk.rearrange("(p j) d -> p j d", j=PACK))
+        def load_table(n, a):
+            nc.sync.dma_start(tabs[n][a][:], (cosn, sinn)[n].rearrange("(p t) u -> p t u", t=PACK)[:, 2 * a, :])
+
+        load_table(0, 0)
+        nc.sync.dma_start(pos[:], offs2)
         nc.sync.dma_start(tok[:], offs)
         for q in range(4):
             nc.sync.dma_start(s_pool[32 * q : 32 * q + 4, :].bitcast(I32), emb_scales[0, 4 * q : 4 * q + 4, :].bitcast(I32))
+        nc.sync.dma_start(w_raw[:], wk.rearrange("(p j) d -> p j d", j=PACK))
+        load_table(0, 1)
         nc.sync.dma_start(e_pool[:], emb_words[0].rearrange("p n t -> p (n t)").bitcast(I32))
-        nc.sync.dma_start(pos[:], offs2)
         for a in range(2):
-            for n, src in enumerate((cosn, sinn)):
-                nc.sync.dma_start(tabs[n][a][:], src.rearrange("(p t) u -> p t u", t=PACK)[:, 2 * a, :])
+            load_table(1, a)
 
+        trig = [sb.tile([P, 2, I], F32, name="trig%d" % n) for n in range(2)]
+
+        def gather_table(n, a):
+            nc.vector.tensor_copy(trig[n][:, a, :], tabs[n][a][:].indirect(pos[:]))
+
+        gather_table(0, 0)
         e_scales = sb.tile([P, I], U8, name="e_scales", align_bytes=64)
         nc.vector.tensor_copy(e_scales[:], s_pool[:].indirect(tok[:]))
-
+        gather_table(0, 1)
         w_codes = sb.tile([P, D], U32, name="w_codes", align_bytes=64)
         w_scales = sb.tile([P, D], U8, name="w_scales", align_bytes=64)
         w_view = w_raw[:].rearrange("p j (m t) -> p m t j", t=PACK)
         for h in range(2):
             w_bf = sb.tile([P, 2, P, PACK], BF16, name="w_bf%d" % h, align_bytes=64)
             dst = w_bf[:].rearrange("p t m j -> p m t j")
-            if h == 0:
-                nc.vector.tensor_copy(dst, w_view[:, :, 0:2, :])
-            else:
-                nc.scalar.copy(dst, w_view[:, :, 2:4, :])
+            nc.scalar.copy(dst, w_view[:, :, 2 * h : 2 * h + 2, :])
             cols = slice(2 * P * h, 2 * P * (h + 1))
             nc.vector.quantize_mx(out=w_codes[:, cols].bitcast(FP8X4), scales=w_scales[:, cols], in_=w_bf[:].rearrange("p t m j -> p (t m j)"))
 
@@ -76,34 +84,51 @@ def tile_attend_freshrope_pl_kernel(tc, emb_words, emb_scales, wk, cosn, sinn, o
                                     rhs=e_codes[:, cols].bitcast(FP8X4), rhs_scale=e_scales[:, cols], start=True, stop=True)
             banks.append(bank)
 
-        trig = [sb.tile([P, 2, I], F32, name="trig%d" % n) for n in range(2)]
         for a in range(2):
-            for n in range(2):
-                nc.vector.tensor_copy(trig[n][:, a, :], tabs[n][a][:].indirect(pos[:]))
+            gather_table(1, a)
 
-        y_bf = sb.tile([P, I, PACK], BF16, name="y_bf", align_bytes=64)
-        y_codes = sb.tile([P, I], U32, name="y_codes", align_bytes=64)
+        y_bf = [sb.tile([P, 2 * CH, PACK], BF16, name="y_bf%d" % h, align_bytes=64) for h in range(2)]
+        y_codes = [sb.tile([P, 2 * CH], U32, name="y_codes%d" % h, align_bytes=64) for h in range(2)]
         y_scales = sb.tile([P, I], U8, name="y_scales", align_bytes=64)
         out_view = out_0.rearrange("(p t) i -> p t i", t=PACK)
+        terms = []
         for c in range(NCH):
             cols = slice(c * CH, (c + 1) * CH)
-            prods = []
-            for n in range(2):
-                prod = sb.tile([P, 2, 2, CH], F32, name="prod%d%d" % (c, n))
-                nc.vector.tensor_tensor(prod[:], banks[c][:].rearrange("p (a e) i -> p a e i", e=2),
-                                        trig[n][:, :, cols].unsqueeze(2).to_broadcast([P, 2, 2, CH]), MULT)
-                prods.append(prod)
-            y = sb.tile([P, 2, 2, CH], F32, name="y%d" % c)
-            eng = nc.vector if c == NCH - 1 else nc.gpsimd
-            eng.tensor_tensor(y[:, :, 0, :], prods[0][:, :, 0, :], prods[1][:, :, 1, :], SUB)
-            eng.tensor_tensor(y[:, :, 1, :], prods[0][:, :, 1, :], prods[1][:, :, 0, :], ADD)
-            nc.sync.dma_start(out_view[:, :, cols], y[:].rearrange("p a e i -> p (a e) i"))
-            nc.scalar.copy(y_bf[:, cols, :].rearrange("p (g i) t -> p g t i", i=4), y[:].rearrange("p a e (g i) -> p g (a e) i", i=4))
+            b = banks[c][:].rearrange("p (a e) i -> p a e i", e=2)
+            if c < 2:
+                cos_terms = sb.tile([P, (1, NCH - 1)[c], 2, 2, CH], F32, name="cos_terms%d" % c, tag="tab1%d" % c)
+            cos_term = cos_terms[:, max(c - 1, 0)]
+            nc.vector.tensor_tensor(cos_term, b, trig[0][:, :, cols].unsqueeze(2).to_broadcast([P, 2, 2, CH]), MULT)
+            sin_term = sb.tile([P, 2, 2, CH], F32, name="sin_term%d" % c)
+            nc.vector.scalar_tensor_tensor(sin_term[:, :, 0, :], b[:, :, 1, :], -1.0, trig[1][:, :, cols], MULT, MULT)
+            nc.vector.tensor_tensor(sin_term[:, :, 1, :], b[:, :, 0, :], trig[1][:, :, cols], MULT)
+            terms.append((cos_term, sin_term))
 
         words = out_1[0].rearrange("p n t -> p (n t)").bitcast(I32)
-        for lo, hi in ((0, 256), (256, 384), (384, 512)):
-            nc.vector.quantize_mx(out=y_codes[:, lo:hi].bitcast(FP8X4), scales=y_scales[:, lo:hi], in_=y_bf[:, lo:hi, :].rearrange("p i t -> p (i t)"))
-        for lo, hi in ((0, 256), (256, 512)):
-            nc.sync.dma_start(words[:, lo:hi], y_codes[:, lo:hi].bitcast(I32))
+        ys = []
+        for c in range(NCH):
+            cols = slice(c * CH, (c + 1) * CH)
+            y = sb.tile([P, 2, 2, CH], F32, name="y%d" % c)
+            eng = nc.gpsimd if c < NG else nc.vector
+            eng.tensor_tensor(y[:].rearrange("p a e i -> p (a e i)"), terms[c][0].rearrange("p a e i -> p (a e i)"),
+                              terms[c][1][:].rearrange("p a e i -> p (a e i)"), ADD)
+            nc.sync.dma_start(out_view[:, :, cols], y[:].rearrange("p a e i -> p (a e) i"))
+            ys.append(y)
+
+        def interleave(c, copy):
+            half = y_bf[c // 2][:, (c % 2) * CH : (c % 2 + 1) * CH, :]
+            copy(half.rearrange("p (g i) t -> p g t i", i=4), ys[c][:].rearrange("p a e (g i) -> p g (a e) i", i=4))
+
+        def quantize(h):
+            cols = slice(2 * CH * h, 2 * CH * (h + 1))
+            nc.vector.quantize_mx(out=y_codes[h][:].bitcast(FP8X4), scales=y_scales[:, cols], in_=y_bf[h][:].rearrange("p i t -> p (i t)"))
+            nc.sync.dma_start(words[:, cols], y_codes[h][:].bitcast(I32))
+
+        for c in range(NCH - 1):
+            interleave(c, nc.scalar.copy)
+        quantize(0)
+        interleave(NCH - 1, nc.vector.tensor_copy)
+        quantize(1)
         for q in range(4):
-            nc.scalar.dma_start(out_2[0, 4 * q : 4 * q + 4, :].bitcast(I32), y_scales[32 * q : 32 * q + 4, :].bitcast(I32))
+            queue = nc.sync if q == 0 else nc.scalar
+            queue.dma_start(out_2[0, 4 * q : 4 * q + 4, :].bitcast(I32), y_scales[32 * q : 32 * q + 4, :].bitcast(I32))

@@ -19,9 +19,7 @@ SUB = mybir.AluOpType.subtract
 
 P = 128
 PACK = 4
-CH = 128
-NCH = I // CH
-NG = 3
+HALF = I // 2
 
 
 def tile_attend_freshrope_pl_kernel(tc, emb_words, emb_scales, wk, cosn, sinn, offs, offs2, out_0, out_1, out_2):
@@ -74,60 +72,59 @@ def tile_attend_freshrope_pl_kernel(tc, emb_words, emb_scales, wk, cosn, sinn, o
         e_codes = sb.tile([P, I], U32, name="e_codes", align_bytes=64)
         nc.vector.tensor_copy(e_codes[:], e_pool[:].bitcast(U32).indirect(tok[:]))
 
+        chunks = [(h, a) for h in range(2) for a in range(2)]
         banks = []
-        for c in range(NCH):
-            bank = ps.tile([P, PACK, CH], F32, name="bank%d" % c)
-            cols = slice(c * CH, (c + 1) * CH)
-            for t in range(PACK):
-                wc = slice(t * P, (t + 1) * P)
-                nc.tensor.matmul_mx(out=bank[:, t, :], lhsT=w_codes[:, wc].bitcast(FP8X4), lhsT_scale=w_scales[:, wc],
+        for c, (h, a) in enumerate(chunks):
+            bank = ps.tile([P, 2, HALF], F32, name="bank%d" % c)
+            cols = slice(h * HALF, (h + 1) * HALF)
+            for e in range(2):
+                wc = slice((2 * a + e) * P, (2 * a + e + 1) * P)
+                nc.tensor.matmul_mx(out=bank[:, e, :], lhsT=w_codes[:, wc].bitcast(FP8X4), lhsT_scale=w_scales[:, wc],
                                     rhs=e_codes[:, cols].bitcast(FP8X4), rhs_scale=e_scales[:, cols], start=True, stop=True)
             banks.append(bank)
 
         for a in range(2):
             gather_table(1, a)
 
-        y_bf = [sb.tile([P, 2 * CH, PACK], BF16, name="y_bf%d" % h, align_bytes=64) for h in range(2)]
-        y_codes = [sb.tile([P, 2 * CH], U32, name="y_codes%d" % h, align_bytes=64) for h in range(2)]
+        y_bf = [sb.tile([P, HALF, PACK], BF16, name="y_bf%d" % h, align_bytes=64) for h in range(2)]
         y_scales = sb.tile([P, I], U8, name="y_scales", align_bytes=64)
+        ys = [sb.tile([P, PACK, HALF], F32, name="y%d" % h) for h in range(2)]
         out_view = out_0.rearrange("(p t) i -> p t i", t=PACK)
-        terms = []
-        for c in range(NCH):
-            cols = slice(c * CH, (c + 1) * CH)
-            b = banks[c][:].rearrange("p (a e) i -> p a e i", e=2)
-            if c < 2:
-                cos_terms = sb.tile([P, (1, NCH - 1)[c], 2, 2, CH], F32, name="cos_terms%d" % c, tag="tab1%d" % c)
-            cos_term = cos_terms[:, max(c - 1, 0)]
-            nc.vector.tensor_tensor(cos_term, b, trig[0][:, :, cols].unsqueeze(2).to_broadcast([P, 2, 2, CH]), MULT)
-            sin_term = sb.tile([P, 2, 2, CH], F32, name="sin_term%d" % c)
-            nc.vector.scalar_tensor_tensor(sin_term[:, :, 0, :], b[:, :, 1, :], -1.0, trig[1][:, :, cols], MULT, MULT)
-            nc.vector.tensor_tensor(sin_term[:, :, 1, :], b[:, :, 0, :], trig[1][:, :, cols], MULT)
-            terms.append((cos_term, sin_term))
-
         words = out_1[0].rearrange("p n t -> p (n t)").bitcast(I32)
-        ys = []
-        for c in range(NCH):
-            cols = slice(c * CH, (c + 1) * CH)
-            y = sb.tile([P, 2, 2, CH], F32, name="y%d" % c)
-            eng = nc.gpsimd if c < NG else nc.vector
-            eng.tensor_tensor(y[:].rearrange("p a e i -> p (a e i)"), terms[c][0].rearrange("p a e i -> p (a e i)"),
-                              terms[c][1][:].rearrange("p a e i -> p (a e i)"), ADD)
-            nc.sync.dma_start(out_view[:, :, cols], y[:].rearrange("p a e i -> p (a e) i"))
-            ys.append(y)
 
-        def interleave(c, copy):
-            half = y_bf[c // 2][:, (c % 2) * CH : (c % 2 + 1) * CH, :]
-            copy(half.rearrange("p (g i) t -> p g t i", i=4), ys[c][:].rearrange("p a e (g i) -> p g (a e) i", i=4))
+        terms = sb.tile([P, len(chunks), 2, 2, HALF], F32, name="terms", tag="tab11")
+        first_cos = sb.tile([P, 2, HALF], F32, name="first_cos", tag="tab10")
+        last_sin = sb.tile([P, 2, HALF], F32, name="last_sin", tag="y_codes0", align_bytes=64)
+        pairs = []
+        for c, (h, a) in enumerate(chunks):
+            cols = slice(h * HALF, (h + 1) * HALF)
+            cos_term = first_cos[:] if c == 0 else terms[:, c, 0]
+            sin_term = last_sin[:] if c == len(chunks) - 1 else terms[:, c, 1]
+            nc.vector.tensor_tensor(cos_term, banks[c][:], trig[0][:, a, cols].unsqueeze(1).to_broadcast([P, 2, HALF]), MULT)
+            nc.vector.scalar_tensor_tensor(sin_term[:, 0, :], banks[c][:, 1, :], -1.0, trig[1][:, a, cols], MULT, MULT)
+            nc.vector.tensor_tensor(sin_term[:, 1, :], banks[c][:, 0, :], trig[1][:, a, cols], MULT)
+            pairs.append((cos_term, sin_term))
+
+        for c, (h, a) in enumerate(chunks):
+            rows = slice(2 * a, 2 * a + 2)
+            eng = nc.gpsimd if c < len(chunks) - 1 else nc.vector
+            eng.tensor_tensor(ys[h][:, rows, :].rearrange("p e i -> p (e i)"), pairs[c][0].rearrange("p e i -> p (e i)"),
+                              pairs[c][1].rearrange("p e i -> p (e i)"), ADD)
+            nc.sync.dma_start(out_view[:, rows, h * HALF : (h + 1) * HALF], ys[h][:, rows, :])
+
+        def interleave(h, lo, hi, copy):
+            copy(y_bf[h][:, lo:hi, :].rearrange("p (g i) t -> p g t i", i=4), ys[h][:, :, lo:hi].rearrange("p t (g i) -> p g t i", i=4))
 
         def quantize(h):
-            cols = slice(2 * CH * h, 2 * CH * (h + 1))
-            nc.vector.quantize_mx(out=y_codes[h][:].bitcast(FP8X4), scales=y_scales[:, cols], in_=y_bf[h][:].rearrange("p i t -> p (i t)"))
-            nc.sync.dma_start(words[:, cols], y_codes[h][:].bitcast(I32))
+            cols = slice(HALF * h, HALF * (h + 1))
+            y_codes = sb.tile([P, HALF], U32, name="y_codes%d" % h, tag="y_codes%d" % h, align_bytes=64)
+            nc.vector.quantize_mx(out=y_codes[:].bitcast(FP8X4), scales=y_scales[:, cols], in_=y_bf[h][:].rearrange("p i t -> p (i t)"))
+            nc.sync.dma_start(words[:, cols], y_codes[:].bitcast(I32))
 
-        for c in range(NCH - 1):
-            interleave(c, nc.scalar.copy)
+        interleave(0, 0, HALF, nc.scalar.copy)
+        interleave(1, 0, HALF // 2, nc.scalar.copy)
         quantize(0)
-        interleave(NCH - 1, nc.vector.tensor_copy)
+        interleave(1, HALF // 2, HALF, nc.vector.tensor_copy)
         quantize(1)
         for q in range(4):
             queue = nc.sync if q == 0 else nc.scalar

@@ -42,8 +42,8 @@ def tile_attend_freshrope_pl_kernel(tc, emb_words, emb_scales, wk, cosn, sinn, o
         load_table(0, 0)
         nc.sync.dma_start(pos[:], offs2)
         nc.sync.dma_start(tok[:], offs)
-        for q in range(4):
-            nc.sync.dma_start(s_pool[32 * q : 32 * q + 4, :].bitcast(I32), emb_scales[0, 4 * q : 4 * q + 4, :].bitcast(I32))
+        for r in range(4):
+            nc.sync.dma_start(s_pool[r:P:32, :].bitcast(I32), emb_scales[0].rearrange("(q r) n -> r q n", r=4)[r].bitcast(I32))
         nc.sync.dma_start(w_raw[:], wk.rearrange("(p j) d -> p j d", j=PACK))
         load_table(0, 1)
         nc.sync.dma_start(e_pool[:], emb_words[0].rearrange("p n t -> p (n t)").bitcast(I32))
@@ -58,17 +58,18 @@ def tile_attend_freshrope_pl_kernel(tc, emb_words, emb_scales, wk, cosn, sinn, o
         gather_table(0, 0)
         e_scales = sb.tile([P, I], U8, name="e_scales", align_bytes=64)
         nc.vector.tensor_copy(e_scales[:], s_pool[:].indirect(tok[:]))
-        gather_table(0, 1)
         w_codes = sb.tile([P, D], U32, name="w_codes", align_bytes=64)
         w_scales = sb.tile([P, D], U8, name="w_scales", align_bytes=64)
         w_view = w_raw[:].rearrange("p j (m t) -> p m t j", t=PACK)
         for h in range(2):
             w_bf = sb.tile([P, 2, P, PACK], BF16, name="w_bf%d" % h, align_bytes=64)
             dst = w_bf[:].rearrange("p t m j -> p m t j")
-            nc.scalar.copy(dst, w_view[:, :, 2 * h : 2 * h + 2, :])
+            copy = (nc.vector.tensor_copy, nc.scalar.copy)[h]
+            copy(dst, w_view[:, :, 2 * h : 2 * h + 2, :])
             cols = slice(2 * P * h, 2 * P * (h + 1))
             nc.vector.quantize_mx(out=w_codes[:, cols].bitcast(FP8X4), scales=w_scales[:, cols], in_=w_bf[:].rearrange("p t m j -> p (t m j)"))
 
+        gather_table(0, 1)
         e_codes = sb.tile([P, I], U32, name="e_codes", align_bytes=64)
         nc.vector.tensor_copy(e_codes[:], e_pool[:].bitcast(U32).indirect(tok[:]))
 

@@ -20,6 +20,8 @@ SUB = mybir.AluOpType.subtract
 P = 128
 PACK = 4
 HALF = I // 2
+QUARTER = I // 4
+LIST_COLS = I // 16
 
 
 def tile_attend_freshrope_pl_kernel(tc, emb_words, emb_scales, wk, cosn, sinn, offs, offs2, out_0, out_1, out_2):
@@ -28,105 +30,145 @@ def tile_attend_freshrope_pl_kernel(tc, emb_words, emb_scales, wk, cosn, sinn, o
         sb = ctx.enter_context(tc.tile_pool(name="sb", bufs=1))
         ps = ctx.enter_context(tc.psum_pool(name="ps", bufs=1))
 
-        tok = sb.tile([P, I // 16], U16, name="tok")
-        pos = sb.tile([P, I // 16], U16, name="pos")
+        tok = sb.tile([P, LIST_COLS], U16, name="tok")
+        pos = sb.tile([P, LIST_COLS], U16, name="pos")
         w_raw = sb.tile([P, PACK, D], F32, name="w_raw")
         e_pool = sb.tile([P, T], I32, name="e_pool", align_bytes=64)
         s_pool = sb.tile([P, T], U8, name="s_pool", align_bytes=64)
         tabs = [[sb.tile([P, U], F32, name="tab%d%d" % (n, a), tag="tab%d%d" % (n, a)) for a in range(2)] for n in range(2)]
 
-        nc.vector.memset(s_pool[:].bitcast(I32), 0)
-        def load_table(n, a):
-            nc.sync.dma_start(tabs[n][a][:], (cosn, sinn)[n].rearrange("(p t) u -> p t u", t=PACK)[:, 2 * a, :])
-
-        load_table(0, 0)
-        nc.sync.dma_start(pos[:], offs2)
+        nc.gpsimd.memset(s_pool[:].bitcast(I32), 0)
         nc.sync.dma_start(tok[:], offs)
+        nc.sync.dma_start(w_raw[:], wk.rearrange("(p j) d -> p j d", j=PACK))
+        nc.sync.dma_start(pos[:], offs2)
         for r in range(4):
             nc.sync.dma_start(s_pool[r:P:32, :].bitcast(I32), emb_scales[0].rearrange("(q r) n -> r q n", r=4)[r].bitcast(I32))
-        nc.sync.dma_start(w_raw[:], wk.rearrange("(p j) d -> p j d", j=PACK))
-        load_table(0, 1)
         nc.sync.dma_start(e_pool[:], emb_words[0].rearrange("p n t -> p (n t)").bitcast(I32))
         for a in range(2):
-            load_table(1, a)
+            for n in range(2):
+                nc.sync.dma_start(tabs[n][a][:], (cosn, sinn)[n].rearrange("(p t) u -> p t u", t=PACK)[:, 2 * a, :])
 
-        trig = [sb.tile([P, 2, I], F32, name="trig%d" % n) for n in range(2)]
+        def slots(h):
+            return slice(h * HALF, (h + 1) * HALF)
 
-        def gather_table(n, a):
-            nc.vector.tensor_copy(trig[n][:, a, :], tabs[n][a][:].indirect(pos[:]))
+        def entries(lst, h):
+            return lst[:, h * LIST_COLS // 2 : (h + 1) * LIST_COLS // 2]
 
-        gather_table(0, 0)
-        e_scales = sb.tile([P, I], U8, name="e_scales", align_bytes=64)
-        nc.vector.tensor_copy(e_scales[:], s_pool[:].indirect(tok[:]))
         w_codes = sb.tile([P, D], U32, name="w_codes", align_bytes=64)
         w_scales = sb.tile([P, D], U8, name="w_scales", align_bytes=64)
         w_view = w_raw[:].rearrange("p j (m t) -> p m t j", t=PACK)
-        for h in range(2):
-            w_bf = sb.tile([P, 2, P, PACK], BF16, name="w_bf%d" % h, align_bytes=64)
-            dst = w_bf[:].rearrange("p t m j -> p m t j")
-            copy = (nc.vector.tensor_copy, nc.scalar.copy)[h]
-            copy(dst, w_view[:, :, 2 * h : 2 * h + 2, :])
-            cols = slice(2 * P * h, 2 * P * (h + 1))
-            nc.vector.quantize_mx(out=w_codes[:, cols].bitcast(FP8X4), scales=w_scales[:, cols], in_=w_bf[:].rearrange("p t m j -> p (t m j)"))
-
-        gather_table(0, 1)
-        e_codes = sb.tile([P, I], U32, name="e_codes", align_bytes=64)
-        nc.vector.tensor_copy(e_codes[:], e_pool[:].bitcast(U32).indirect(tok[:]))
-
-        chunks = [(h, a) for h in range(2) for a in range(2)]
-        banks = []
-        for c, (h, a) in enumerate(chunks):
-            bank = ps.tile([P, 2, HALF], F32, name="bank%d" % c)
-            cols = slice(h * HALF, (h + 1) * HALF)
-            for e in range(2):
-                wc = slice((2 * a + e) * P, (2 * a + e + 1) * P)
-                nc.tensor.matmul_mx(out=bank[:, e, :], lhsT=w_codes[:, wc].bitcast(FP8X4), lhsT_scale=w_scales[:, wc],
-                                    rhs=e_codes[:, cols].bitcast(FP8X4), rhs_scale=e_scales[:, cols], start=True, stop=True)
-            banks.append(bank)
-
+        w_bf = [sb.tile([P, 2, P, PACK], BF16, name="w_bf%d" % a, align_bytes=64) for a in range(2)]
         for a in range(2):
-            gather_table(1, a)
+            (nc.vector.tensor_copy, nc.scalar.copy)[a](w_bf[a][:].rearrange("p t m j -> p m t j"), w_view[:, :, 2 * a : 2 * a + 2, :])
+
+        def quantize_w(a):
+            cols = slice(2 * P * a, 2 * P * (a + 1))
+            nc.vector.quantize_mx(out=w_codes[:, cols].bitcast(FP8X4), scales=w_scales[:, cols], in_=w_bf[a][:].rearrange("p t m j -> p (t m j)"))
+
+        e_scales = sb.tile([P, I], U8, name="e_scales", align_bytes=64)
+        e_codes = sb.tile([P, I], U32, name="e_codes", align_bytes=64)
+        nc.vector.tensor_copy(e_scales[:], s_pool[:].indirect(tok[:]))
+        quantize_w(0)
+        quantize_w(1)
+        for h in range(2):
+            nc.vector.tensor_copy(e_codes[:, slots(h)], e_pool[:].bitcast(U32).indirect(entries(tok, h)))
+
+        trig = [[sb.tile([P, I], F32, name="trig%d%d" % (n, a)) for a in range(2)] for n in range(2)]
+
+        def gather_half(n, a, h):
+            nc.vector.tensor_copy(trig[n][a][:, slots(h)], tabs[n][a][:].indirect(entries(pos, h)))
+
+        def gather(n, a):
+            nc.vector.tensor_copy(trig[n][a][:], tabs[n][a][:].indirect(pos[:]))
+
+        banks = {}
+        for h in range(2):
+            for a in range(2):
+                bank = ps.tile([P, 2, HALF], F32, name="bank%d%d" % (a, h))
+                for e in range(2):
+                    wc = slice((2 * a + e) * P, (2 * a + e + 1) * P)
+                    nc.tensor.matmul_mx(out=bank[:, e, :], lhsT=w_codes[:, wc].bitcast(FP8X4), lhsT_scale=w_scales[:, wc],
+                                        rhs=e_codes[:, slots(h)].bitcast(FP8X4), rhs_scale=e_scales[:, slots(h)], start=True, stop=True)
+                banks[a, h] = bank
+
+        on_gpsimd = [(0, 0), (0, 1), (1, 0)]
+        b_sb = {}
+        for a, h in on_gpsimd:
+            b_sb[a, h] = sb.tile([P, 2, HALF], F32, name="b_sb%d%d" % (a, h))
+            nc.scalar.copy(b_sb[a, h][:], banks[a, h][:])
+
+        terms10 = sb.tile([P, 2, 2, HALF], F32, name="terms10", tag="y1")
+        cos11 = sb.tile([P, 2, HALF], F32, name="cos11", tag="tab11")
+        cos_t = {(0, h): sb.tile([P, 2, HALF], F32, name="cos0%d" % h)[:] for h in range(2)}
+        sin_t = {c: sb.tile([P, 2, HALF], F32, name="sin%d%d" % c)[:] for c in ((0, 0), (0, 1), (1, 1))}
+        cos_t[1, 0], sin_t[1, 0], cos_t[1, 1] = terms10[:, 0], terms10[:, 1], cos11[:]
+
+        def cos_term(a, h):
+            cos = trig[0][a][:, slots(h)].unsqueeze(1).to_broadcast([P, 2, HALF])
+            if (a, h) in on_gpsimd:
+                nc.gpsimd.tensor_tensor(cos_t[a, h], b_sb[a, h][:], cos, MULT)
+            else:
+                nc.vector.tensor_tensor(cos_t[a, h], banks[a, h][:], cos, MULT)
+
+        def sin_term(a, h):
+            sin = trig[1][a][:, slots(h)]
+            nc.vector.scalar_tensor_tensor(sin_t[a, h][:, 0, :], banks[a, h][:, 1, :], -1.0, sin, MULT, MULT)
+            nc.vector.tensor_tensor(sin_t[a, h][:, 1, :], banks[a, h][:, 0, :], sin, MULT)
+
+        out_view = out_0.rearrange("(p t) i -> p t i", t=PACK)
+        words = out_1[0].rearrange("p n t -> p (n t)").bitcast(I32)
+        ys = {}
+
+        def add(eng, a, h, lo, hi):
+            rows = slice(2 * a, 2 * a + 2)
+            eng.tensor_tensor(ys[h][:, rows, lo:hi], cos_t[a, h][:, :, lo:hi], sin_t[a, h][:, :, lo:hi], ADD)
+
+        def store(a, h):
+            rows = slice(2 * a, 2 * a + 2)
+            nc.sync.dma_start(out_view[:, rows, slots(h)], ys[h][:, rows, :])
+
+        gather_half(0, 0, 0)
+        gather_half(0, 0, 1)
+        cos_term(0, 0)
+        cos_term(0, 1)
+        gather(1, 0)
+        sin_term(0, 0)
+        sin_term(0, 1)
+        ys[0] = sb.tile([P, PACK, HALF], F32, name="y0")
+        add(nc.gpsimd, 0, 0, 0, HALF)
+        store(0, 0)
+        gather(0, 1)
+        cos_term(1, 0)
+        gather_half(1, 1, 0)
+        gather_half(1, 1, 1)
+        sin_term(1, 0)
+        add(nc.gpsimd, 1, 0, 0, HALF)
+        store(1, 0)
+        cos_term(1, 1)
+        sin_term(1, 1)
+        ys[1] = sb.tile([P, PACK, HALF], F32, name="y1", tag="y1")
+        add(nc.vector, 0, 1, 0, HALF)
+        store(0, 1)
+        add(nc.vector, 1, 1, 0, QUARTER)
+        add(nc.vector, 1, 1, QUARTER, HALF)
+        store(1, 1)
 
         y_bf = [sb.tile([P, HALF, PACK], BF16, name="y_bf%d" % h, align_bytes=64) for h in range(2)]
         y_scales = sb.tile([P, I], U8, name="y_scales", align_bytes=64)
-        ys = [sb.tile([P, PACK, HALF], F32, name="y%d" % h) for h in range(2)]
-        out_view = out_0.rearrange("(p t) i -> p t i", t=PACK)
-        words = out_1[0].rearrange("p n t -> p (n t)").bitcast(I32)
-
-        terms = sb.tile([P, len(chunks), 2, 2, HALF], F32, name="terms", tag="tab11")
-        first_cos = sb.tile([P, 2, HALF], F32, name="first_cos", tag="tab10")
-        last_sin = sb.tile([P, 2, HALF], F32, name="last_sin", tag="y_codes0", align_bytes=64)
-        pairs = []
-        for c, (h, a) in enumerate(chunks):
-            cols = slice(h * HALF, (h + 1) * HALF)
-            cos_term = first_cos[:] if c == 0 else terms[:, c, 0]
-            sin_term = last_sin[:] if c == len(chunks) - 1 else terms[:, c, 1]
-            nc.vector.tensor_tensor(cos_term, banks[c][:], trig[0][:, a, cols].unsqueeze(1).to_broadcast([P, 2, HALF]), MULT)
-            nc.vector.scalar_tensor_tensor(sin_term[:, 0, :], banks[c][:, 1, :], -1.0, trig[1][:, a, cols], MULT, MULT)
-            nc.vector.tensor_tensor(sin_term[:, 1, :], banks[c][:, 0, :], trig[1][:, a, cols], MULT)
-            pairs.append((cos_term, sin_term))
-
-        for c, (h, a) in enumerate(chunks):
-            rows = slice(2 * a, 2 * a + 2)
-            eng = nc.gpsimd if c < len(chunks) - 1 else nc.vector
-            eng.tensor_tensor(ys[h][:, rows, :].rearrange("p e i -> p (e i)"), pairs[c][0].rearrange("p e i -> p (e i)"),
-                              pairs[c][1].rearrange("p e i -> p (e i)"), ADD)
-            nc.sync.dma_start(out_view[:, rows, h * HALF : (h + 1) * HALF], ys[h][:, rows, :])
 
         def interleave(h, lo, hi, copy):
             copy(y_bf[h][:, lo:hi, :].rearrange("p (g i) t -> p g t i", i=4), ys[h][:, :, lo:hi].rearrange("p t (g i) -> p g t i", i=4))
 
         def quantize(h):
-            cols = slice(HALF * h, HALF * (h + 1))
-            y_codes = sb.tile([P, HALF], U32, name="y_codes%d" % h, tag="y_codes%d" % h, align_bytes=64)
-            nc.vector.quantize_mx(out=y_codes[:].bitcast(FP8X4), scales=y_scales[:, cols], in_=y_bf[h][:].rearrange("p i t -> p (i t)"))
-            nc.sync.dma_start(words[:, cols], y_codes[:].bitcast(I32))
+            y_codes = sb.tile([P, HALF], U32, name="y_codes%d" % h, align_bytes=64)
+            nc.vector.quantize_mx(out=y_codes[:].bitcast(FP8X4), scales=y_scales[:, slots(h)], in_=y_bf[h][:].rearrange("p i t -> p (i t)"))
+            nc.sync.dma_start(words[:, slots(h)], y_codes[:].bitcast(I32))
 
         interleave(0, 0, HALF, nc.scalar.copy)
-        interleave(1, 0, HALF // 2, nc.scalar.copy)
+        interleave(1, 0, QUARTER, nc.scalar.copy)
+        interleave(1, QUARTER, HALF, nc.vector.tensor_copy)
         quantize(0)
-        interleave(1, HALF // 2, HALF, nc.vector.tensor_copy)
         quantize(1)
         for q in range(4):
-            queue = nc.sync if q == 0 else nc.scalar
+            queue = nc.sync if q < 2 else nc.scalar
             queue.dma_start(out_2[0, 4 * q : 4 * q + 4, :].bitcast(I32), y_scales[32 * q : 32 * q + 4, :].bitcast(I32))

@@ -1,6 +1,7 @@
 from contextlib import ExitStack
 
 import concourse.mybir as mybir
+from concourse.masks import make_identity
 
 K, T, I, D, U = 512, 2048, 512, 512, 1024
 FLOPS = 2 * K * D * I
@@ -22,6 +23,7 @@ PACK = 4
 HALF = I // 2
 QUARTER = I // 4
 LIST_COLS = I // 16
+GP_ADD = 192
 
 
 def tile_attend_freshrope_pl_kernel(tc, emb_words, emb_scales, wk, cosn, sinn, offs, offs2, out_0, out_1, out_2):
@@ -36,137 +38,152 @@ def tile_attend_freshrope_pl_kernel(tc, emb_words, emb_scales, wk, cosn, sinn, o
         e_pool = sb.tile([P, T], I32, name="e_pool", align_bytes=64)
         s_pool = sb.tile([P, T], U8, name="s_pool", align_bytes=64)
         tabs = [[sb.tile([P, U], F32, name="tab%d%d" % (n, a), tag="tab%d%d" % (n, a)) for a in range(2)] for n in range(2)]
+        ident = sb.tile([P, P], F32, name="ident")
 
-        nc.gpsimd.memset(s_pool[:].bitcast(I32), 0)
-        nc.sync.dma_start(tok[:], offs)
-        nc.sync.dma_start(w_raw[:], wk.rearrange("(p j) d -> p j d", j=PACK))
+        def load_table(n, a):
+            nc.sync.dma_start(tabs[n][a][:], (cosn, sinn)[n].rearrange("(p t) u -> p t u", t=PACK)[:, 2 * a, :])
+
+        nc.vector.memset(s_pool[:].bitcast(I32), 0)
+        make_identity(nc, ident[:])
+        load_table(0, 0)
         nc.sync.dma_start(pos[:], offs2)
+        nc.sync.dma_start(tok[:], offs)
         for r in range(4):
             nc.sync.dma_start(s_pool[r:P:32, :].bitcast(I32), emb_scales[0].rearrange("(q r) n -> r q n", r=4)[r].bitcast(I32))
+        nc.sync.dma_start(w_raw[:], wk.rearrange("(p j) d -> p j d", j=PACK))
+        load_table(0, 1)
         nc.sync.dma_start(e_pool[:], emb_words[0].rearrange("p n t -> p (n t)").bitcast(I32))
-        for a in range(2):
-            for n in range(2):
-                nc.sync.dma_start(tabs[n][a][:], (cosn, sinn)[n].rearrange("(p t) u -> p t u", t=PACK)[:, 2 * a, :])
+        load_table(1, 0)
+        load_table(1, 1)
 
         def slots(h):
             return slice(h * HALF, (h + 1) * HALF)
 
+        def block(g):
+            return slice(g * P, (g + 1) * P)
+
         def entries(lst, h):
             return lst[:, h * LIST_COLS // 2 : (h + 1) * LIST_COLS // 2]
+
+        trig = [sb.tile([P, 2, I], F32, name="trig%d" % n) for n in range(2)]
+        turned = [[ps.tile([P, 2, P], F32, name="turned%d%d" % (n, a)) for a in range(2)] for n in range(2)]
+
+        def turn(n, a):
+            for g in range(2):
+                nc.tensor.transpose(turned[n][a][:, g, :], trig[n][:, a, block(g)], ident[:])
+
+        def gather(n, a):
+            nc.vector.tensor_copy(trig[n][:, a, :], tabs[n][a][:].indirect(pos[:]))
+            turn(n, a)
+
+        gather(0, 0)
+        e_scales = sb.tile([P, I], U8, name="e_scales", align_bytes=64)
+        nc.vector.tensor_copy(e_scales[:], s_pool[:].indirect(tok[:]))
 
         w_codes = sb.tile([P, D], U32, name="w_codes", align_bytes=64)
         w_scales = sb.tile([P, D], U8, name="w_scales", align_bytes=64)
         w_view = w_raw[:].rearrange("p j (m t) -> p m t j", t=PACK)
-        w_bf = [sb.tile([P, 2, P, PACK], BF16, name="w_bf%d" % a, align_bytes=64) for a in range(2)]
         for a in range(2):
-            (nc.vector.tensor_copy, nc.scalar.copy)[a](w_bf[a][:].rearrange("p t m j -> p m t j"), w_view[:, :, 2 * a : 2 * a + 2, :])
-
-        def quantize_w(a):
+            w_bf = sb.tile([P, 2, P, PACK], BF16, name="w_bf%d" % a, align_bytes=64)
+            (nc.vector.tensor_copy, nc.scalar.copy)[a](w_bf[:].rearrange("p t m j -> p m t j"), w_view[:, :, 2 * a : 2 * a + 2, :])
             cols = slice(2 * P * a, 2 * P * (a + 1))
-            nc.vector.quantize_mx(out=w_codes[:, cols].bitcast(FP8X4), scales=w_scales[:, cols], in_=w_bf[a][:].rearrange("p t m j -> p (t m j)"))
+            nc.vector.quantize_mx(out=w_codes[:, cols].bitcast(FP8X4), scales=w_scales[:, cols], in_=w_bf[:].rearrange("p t m j -> p (t m j)"))
 
-        e_scales = sb.tile([P, I], U8, name="e_scales", align_bytes=64)
+        gather(0, 1)
         e_codes = sb.tile([P, I], U32, name="e_codes", align_bytes=64)
-        nc.vector.tensor_copy(e_scales[:], s_pool[:].indirect(tok[:]))
-        quantize_w(0)
-        quantize_w(1)
         for h in range(2):
             nc.vector.tensor_copy(e_codes[:, slots(h)], e_pool[:].bitcast(U32).indirect(entries(tok, h)))
 
-        trig = [[sb.tile([P, I], F32, name="trig%d%d" % (n, a)) for a in range(2)] for n in range(2)]
+        def product(out, w_cols, e_cols, w_moves):
+            w = (w_codes[:, w_cols].bitcast(FP8X4), w_scales[:, w_cols])
+            e = (e_codes[:, e_cols].bitcast(FP8X4), e_scales[:, e_cols])
+            still, moving = (e, w) if w_moves else (w, e)
+            nc.tensor.matmul_mx(out=out, lhsT=still[0], lhsT_scale=still[1], rhs=moving[0], rhs_scale=moving[1], start=True, stop=True)
 
-        def gather_half(n, a, h):
-            nc.vector.tensor_copy(trig[n][a][:, slots(h)], tabs[n][a][:].indirect(entries(pos, h)))
+        b_turned = sb.tile([P, PACK, 2, P], F32, name="b_turned")
+        for g in range(2):
+            bank = ps.tile([P, PACK, P], F32, name="bt%d" % g, tag="block%d" % g)
+            product(bank[:].rearrange("p t m -> p (t m)"), slice(0, D), block(g), True)
+            nc.scalar.copy(b_turned[:, :, g, :], bank[:])
+        banks = [ps.tile([P, 2, HALF], F32, name="bank%d" % a) for a in range(2)]
+        b_plain = sb.tile([P, 2, 2, HALF], F32, name="b_plain")
+        for a in range(2):
+            for e in range(2):
+                product(banks[a][:, e, :], block(2 * a + e), slots(1), False)
+            nc.scalar.copy(b_plain[:, a], banks[a][:])
 
-        def gather(n, a):
-            nc.vector.tensor_copy(trig[n][a][:], tabs[n][a][:].indirect(pos[:]))
+        gather(1, 0)
+        for h in (1, 0):
+            nc.vector.tensor_copy(trig[1][:, 1, slots(h)], tabs[1][1][:].indirect(entries(pos, h)))
+        turn(1, 1)
 
-        banks = {}
-        for h in range(2):
-            for a in range(2):
-                bank = ps.tile([P, 2, HALF], F32, name="bank%d%d" % (a, h))
-                for e in range(2):
-                    wc = slice((2 * a + e) * P, (2 * a + e + 1) * P)
-                    nc.tensor.matmul_mx(out=bank[:, e, :], lhsT=w_codes[:, wc].bitcast(FP8X4), lhsT_scale=w_scales[:, wc],
-                                        rhs=e_codes[:, slots(h)].bitcast(FP8X4), rhs_scale=e_scales[:, slots(h)], start=True, stop=True)
-                banks[a, h] = bank
-
-        on_gpsimd = [(0, 0), (0, 1), (1, 0)]
-        b_sb = {}
-        for a, h in on_gpsimd:
-            b_sb[a, h] = sb.tile([P, 2, HALF], F32, name="b_sb%d%d" % (a, h))
-            nc.scalar.copy(b_sb[a, h][:], banks[a, h][:])
-
-        terms10 = sb.tile([P, 2, 2, HALF], F32, name="terms10", tag="y1")
-        cos11 = sb.tile([P, 2, HALF], F32, name="cos11", tag="tab11")
-        cos_t = {(0, h): sb.tile([P, 2, HALF], F32, name="cos0%d" % h)[:] for h in range(2)}
-        sin_t = {c: sb.tile([P, 2, HALF], F32, name="sin%d%d" % c)[:] for c in ((0, 0), (0, 1), (1, 1))}
-        cos_t[1, 0], sin_t[1, 0], cos_t[1, 1] = terms10[:, 0], terms10[:, 1], cos11[:]
-
-        def cos_term(a, h):
-            cos = trig[0][a][:, slots(h)].unsqueeze(1).to_broadcast([P, 2, HALF])
-            if (a, h) in on_gpsimd:
-                nc.gpsimd.tensor_tensor(cos_t[a, h], b_sb[a, h][:], cos, MULT)
-            else:
-                nc.vector.tensor_tensor(cos_t[a, h], banks[a, h][:], cos, MULT)
-
-        def sin_term(a, h):
-            sin = trig[1][a][:, slots(h)]
-            nc.vector.scalar_tensor_tensor(sin_t[a, h][:, 0, :], banks[a, h][:, 1, :], -1.0, sin, MULT, MULT)
-            nc.vector.tensor_tensor(sin_t[a, h][:, 1, :], banks[a, h][:, 0, :], sin, MULT)
-
+        ys = sb.tile([P, PACK, I], F32, name="ys")
+        terms = sb.tile([P, 7, 2, HALF], F32, name="terms", tag="tab11")
+        cos_plain = terms[:, 4:6]
+        sin_plain = [terms[:, 6], ys[:, 0:2, slots(1)]]
         out_view = out_0.rearrange("(p t) i -> p t i", t=PACK)
         words = out_1[0].rearrange("p n t -> p (n t)").bitcast(I32)
-        ys = {}
-
-        def add(eng, a, h, lo, hi):
-            rows = slice(2 * a, 2 * a + 2)
-            eng.tensor_tensor(ys[h][:, rows, lo:hi], cos_t[a, h][:, :, lo:hi], sin_t[a, h][:, :, lo:hi], ADD)
 
         def store(a, h):
-            rows = slice(2 * a, 2 * a + 2)
-            nc.sync.dma_start(out_view[:, rows, slots(h)], ys[h][:, rows, :])
+            nc.sync.dma_start(out_view[:, 2 * a : 2 * a + 2, slots(h)], ys[:, 2 * a : 2 * a + 2, slots(h)])
 
-        gather_half(0, 0, 0)
-        gather_half(0, 0, 1)
-        cos_term(0, 0)
-        cos_term(0, 1)
-        gather(1, 0)
-        sin_term(0, 0)
-        sin_term(0, 1)
-        ys[0] = sb.tile([P, PACK, HALF], F32, name="y0")
-        add(nc.gpsimd, 0, 0, 0, HALF)
-        store(0, 0)
-        gather(0, 1)
-        cos_term(1, 0)
-        gather_half(1, 1, 0)
-        gather_half(1, 1, 1)
-        sin_term(1, 0)
-        add(nc.gpsimd, 1, 0, 0, HALF)
-        store(1, 0)
-        cos_term(1, 1)
-        sin_term(1, 1)
-        ys[1] = sb.tile([P, PACK, HALF], F32, name="y1", tag="y1")
-        add(nc.vector, 0, 1, 0, HALF)
-        store(0, 1)
-        add(nc.vector, 1, 1, 0, QUARTER)
-        add(nc.vector, 1, 1, QUARTER, HALF)
-        store(1, 1)
+        def sin_term_plain(a):
+            sin = trig[1][:, a, slots(1)]
+            nc.vector.scalar_tensor_tensor(sin_plain[a][:, 0, :], banks[a][:, 1, :], -1.0, sin, MULT, MULT)
+            nc.vector.tensor_tensor(sin_plain[a][:, 1, :], banks[a][:, 0, :], sin, MULT)
 
-        y_bf = [sb.tile([P, HALF, PACK], BF16, name="y_bf%d" % h, align_bytes=64) for h in range(2)]
+        sums = [ps.tile([P, PACK, P], F32, name="sum%d" % g, tag="block%d" % g) for g in range(2)]
+
+        def terms_turned(a):
+            b = b_turned[:, 2 * a : 2 * a + 2].rearrange("p e g m -> p e (g m)")
+            cos, sin = (turned[n][a][:].rearrange("p g m -> p (g m)") for n in range(2))
+            cos_term, sin_term = terms[:, 2 * a], terms[:, 2 * a + 1]
+            nc.vector.tensor_tensor(cos_term, cos.unsqueeze(1).to_broadcast([P, 2, HALF]), b, MULT)
+            nc.vector.scalar_tensor_tensor(sin_term[:, 0, :], sin, -1.0, b[:, 1, :], MULT, MULT)
+            nc.vector.tensor_tensor(sin_term[:, 1, :], sin, b[:, 0, :], MULT)
+            for n, term in enumerate((cos_term, sin_term)):
+                for g in range(2):
+                    for e in range(2):
+                        nc.tensor.matmul(sums[g][:, 2 * a + e, :], term[:, e, block(g)], ident[:], is_transpose=True,
+                                         start=(n == 0 and e == 0), stop=(n == 1 and e == 1))
+
+        def copy_out(a):
+            for g in range(2):
+                nc.scalar.copy(ys[:, 2 * a : 2 * a + 2, block(g)], sums[g][:, 2 * a : 2 * a + 2, :])
+            store(a, 0)
+
+        y_bf = sb.tile([P, I, PACK], BF16, name="y_bf", align_bytes=64)
         y_scales = sb.tile([P, I], U8, name="y_scales", align_bytes=64)
 
-        def interleave(h, lo, hi, copy):
-            copy(y_bf[h][:, lo:hi, :].rearrange("p (g i) t -> p g t i", i=4), ys[h][:, :, lo:hi].rearrange("p t (g i) -> p g t i", i=4))
+        nc.gpsimd.tensor_tensor(cos_plain, b_plain[:], trig[0][:, :, slots(1)].unsqueeze(2).to_broadcast([P, 2, 2, HALF]), MULT)
+        sin_term_plain(1)
+        nc.gpsimd.tensor_tensor(ys[:, 2:4, HALF : HALF + GP_ADD], cos_plain[:, 1, :, :GP_ADD], sin_plain[1][:, :, :GP_ADD], ADD)
+        terms_turned(0)
+        copy_out(0)
+        terms_turned(1)
+        for g in range(2):
+            nc.scalar.copy(y_bf[:, block(g), :], sums[g][:].rearrange("p t i -> p i t"))
+        copy_out(1)
+        sin_term_plain(0)
+
+        def add_plain(a, lo, hi):
+            nc.vector.tensor_tensor(ys[:, 2 * a : 2 * a + 2, HALF + lo : HALF + hi], cos_plain[:, a, :, lo:hi], sin_plain[a][:, :, lo:hi], ADD)
+
+        def round_plain(g):
+            nc.vector.tensor_copy(y_bf[:, block(g), :].rearrange("p (c i) t -> p c t i", i=4), ys[:, :, block(g)].rearrange("p t (c i) -> p c t i", i=4))
 
         def quantize(h):
             y_codes = sb.tile([P, HALF], U32, name="y_codes%d" % h, align_bytes=64)
-            nc.vector.quantize_mx(out=y_codes[:].bitcast(FP8X4), scales=y_scales[:, slots(h)], in_=y_bf[h][:].rearrange("p i t -> p (i t)"))
+            nc.vector.quantize_mx(out=y_codes[:].bitcast(FP8X4), scales=y_scales[:, slots(h)], in_=y_bf[:, slots(h), :].rearrange("p i t -> p (i t)"))
             nc.sync.dma_start(words[:, slots(h)], y_codes[:].bitcast(I32))
 
-        interleave(0, 0, HALF, nc.scalar.copy)
-        interleave(1, 0, QUARTER, nc.scalar.copy)
-        interleave(1, QUARTER, HALF, nc.vector.tensor_copy)
+        add_plain(0, 0, QUARTER)
+        add_plain(1, GP_ADD, HALF)
+        store(1, 1)
+        add_plain(0, QUARTER, HALF)
+        store(0, 1)
+        round_plain(2)
+        round_plain(3)
         quantize(0)
         quantize(1)
         for q in range(4):

@@ -161,9 +161,9 @@ def tile_attend_freshrope_pl_kernel(tc, emb_words, emb_scales, wk, cosn, sinn, o
         terms_turned(0)
         copy_out(0)
         terms_turned(1)
+        copy_out(1)
         for g in range(2):
             nc.scalar.copy(y_bf[:, block(g), :], sums[g][:].rearrange("p t i -> p i t"))
-        copy_out(1)
         sin_term_plain(0)
 
         def add_plain(a, lo, hi):
@@ -184,8 +184,8 @@ def tile_attend_freshrope_pl_kernel(tc, emb_words, emb_scales, wk, cosn, sinn, o
         store(0, 1)
         round_plain(2)
         round_plain(3)
-        quantize(0)
         quantize(1)
+        quantize(0)
         for q in range(4):
             queue = nc.sync if q < 2 else nc.scalar
             queue.dma_start(out_2[0, 4 * q : 4 * q + 4, :].bitcast(I32), y_scales[32 * q : 32 * q + 4, :].bitcast(I32))

@@ -23,7 +23,6 @@ PACK = 4
 HALF = I // 2
 QUARTER = I // 4
 LIST_COLS = I // 16
-GP_ADD = 192
 
 
 def tile_attend_freshrope_pl_kernel(tc, emb_words, emb_scales, wk, cosn, sinn, offs, offs2, out_0, out_1, out_2):
@@ -127,10 +126,12 @@ def tile_attend_freshrope_pl_kernel(tc, emb_words, emb_scales, wk, cosn, sinn, o
         def store(a, h):
             nc.sync.dma_start(out_view[:, 2 * a : 2 * a + 2, slots(h)], ys[:, 2 * a : 2 * a + 2, slots(h)])
 
-        def sin_term_plain(a):
+        def sin_term_plain(a, e):
             sin = trig[1][:, a, slots(1)]
-            nc.vector.scalar_tensor_tensor(sin_plain[a][:, 0, :], banks[a][:, 1, :], -1.0, sin, MULT, MULT)
-            nc.vector.tensor_tensor(sin_plain[a][:, 1, :], banks[a][:, 0, :], sin, MULT)
+            if e == 0:
+                nc.vector.scalar_tensor_tensor(sin_plain[a][:, 0, :], banks[a][:, 1, :], -1.0, sin, MULT, MULT)
+            else:
+                nc.vector.tensor_tensor(sin_plain[a][:, 1, :], banks[a][:, 0, :], sin, MULT)
 
         sums = [ps.tile([P, PACK, P], F32, name="sum%d" % g, tag="block%d" % g) for g in range(2)]
 
@@ -142,13 +143,13 @@ def tile_attend_freshrope_pl_kernel(tc, emb_words, emb_scales, wk, cosn, sinn, o
             nc.vector.scalar_tensor_tensor(sin_term[:, 0, :], sin, -1.0, b[:, 1, :], MULT, MULT)
             nc.vector.tensor_tensor(sin_term[:, 1, :], sin, b[:, 0, :], MULT)
             for n, term in enumerate((cos_term, sin_term)):
-                for g in range(2):
+                for g in (1, 0):
                     for e in range(2):
                         nc.tensor.matmul(sums[g][:, 2 * a + e, :], term[:, e, block(g)], ident[:], is_transpose=True,
                                          start=(n == 0 and e == 0), stop=(n == 1 and e == 1))
 
         def copy_out(a):
-            for g in range(2):
+            for g in (1, 0):
                 nc.scalar.copy(ys[:, 2 * a : 2 * a + 2, block(g)], sums[g][:, 2 * a : 2 * a + 2, :])
             store(a, 0)
 
@@ -156,15 +157,17 @@ def tile_attend_freshrope_pl_kernel(tc, emb_words, emb_scales, wk, cosn, sinn, o
         y_scales = sb.tile([P, I], U8, name="y_scales", align_bytes=64)
 
         nc.gpsimd.tensor_tensor(cos_plain, b_plain[:], trig[0][:, :, slots(1)].unsqueeze(2).to_broadcast([P, 2, 2, HALF]), MULT)
-        sin_term_plain(1)
-        nc.gpsimd.tensor_tensor(ys[:, 2:4, HALF : HALF + GP_ADD], cos_plain[:, 1, :, :GP_ADD], sin_plain[1][:, :, :GP_ADD], ADD)
+        sin_term_plain(1, 0)
+        nc.gpsimd.tensor_tensor(ys[:, 2, slots(1)], cos_plain[:, 1, 0], sin_plain[1][:, 0], ADD)
         terms_turned(0)
         copy_out(0)
         terms_turned(1)
         copy_out(1)
-        for g in range(2):
+        for g in (1, 0):
             nc.scalar.copy(y_bf[:, block(g), :], sums[g][:].rearrange("p t i -> p i t"))
-        sin_term_plain(0)
+        sin_term_plain(1, 1)
+        sin_term_plain(0, 0)
+        sin_term_plain(0, 1)
 
         def add_plain(a, lo, hi):
             nc.vector.tensor_tensor(ys[:, 2 * a : 2 * a + 2, HALF + lo : HALF + hi], cos_plain[:, a, :, lo:hi], sin_plain[a][:, :, lo:hi], ADD)
@@ -172,20 +175,26 @@ def tile_attend_freshrope_pl_kernel(tc, emb_words, emb_scales, wk, cosn, sinn, o
         def round_plain(g):
             nc.vector.tensor_copy(y_bf[:, block(g), :].rearrange("p (c i) t -> p c t i", i=4), ys[:, :, block(g)].rearrange("p t (c i) -> p c t i", i=4))
 
-        def quantize(h):
-            y_codes = sb.tile([P, HALF], U32, name="y_codes%d" % h, align_bytes=64)
-            nc.vector.quantize_mx(out=y_codes[:].bitcast(FP8X4), scales=y_scales[:, slots(h)], in_=y_bf[:, slots(h), :].rearrange("p i t -> p (i t)"))
-            nc.sync.dma_start(words[:, slots(h)], y_codes[:].bitcast(I32))
+        y_codes = sb.tile([P, I], U32, name="y_codes", align_bytes=64)
 
-        add_plain(0, 0, QUARTER)
-        add_plain(1, GP_ADD, HALF)
+        def quantize(cols):
+            nc.vector.quantize_mx(out=y_codes[:, cols].bitcast(FP8X4), scales=y_scales[:, cols], in_=y_bf[:, cols, :].rearrange("p i t -> p (i t)"))
+
+        def store_codes(cols):
+            nc.sync.dma_start(words[:, cols], y_codes[:, cols].bitcast(I32))
+
+        nc.vector.tensor_tensor(ys[:, 3, slots(1)], cos_plain[:, 1, 1], sin_plain[1][:, 1], ADD)
         store(1, 1)
+        add_plain(0, 0, QUARTER)
         add_plain(0, QUARTER, HALF)
         store(0, 1)
         round_plain(2)
         round_plain(3)
-        quantize(1)
-        quantize(0)
+        quantize(block(1))
+        quantize(slots(1))
+        store_codes(slots(1))
+        quantize(block(0))
+        store_codes(slots(0))
         for q in range(4):
             queue = nc.sync if q < 2 else nc.scalar
             queue.dma_start(out_2[0, 4 * q : 4 * q + 4, :].bitcast(I32), y_scales[32 * q : 32 * q + 4, :].bitcast(I32))

@@ -23,6 +23,7 @@ PACK = 4
 HALF = I // 2
 QUARTER = I // 4
 LIST_COLS = I // 16
+GP_SLOTS = 128
 
 
 def tile_attend_freshrope_pl_kernel(tc, emb_words, emb_scales, wk, cosn, sinn, offs, offs2, out_0, out_1, out_2):
@@ -65,11 +66,11 @@ def tile_attend_freshrope_pl_kernel(tc, emb_words, emb_scales, wk, cosn, sinn, o
             return lst[:, h * LIST_COLS // 2 : (h + 1) * LIST_COLS // 2]
 
         trig = [sb.tile([P, 2, I], F32, name="trig%d" % n) for n in range(2)]
-        turned = [[ps.tile([P, 2, P], F32, name="turned%d%d" % (n, a)) for a in range(2)] for n in range(2)]
+        turned = [ps.tile([P, 2, 2, P], F32, name="turned%d" % n) for n in range(2)]
 
         def turn(n, a):
-            for g in range(2):
-                nc.tensor.transpose(turned[n][a][:, g, :], trig[n][:, a, block(g)], ident[:])
+            for g in (1, 0):
+                nc.tensor.transpose(turned[n][:, g, a, :], trig[n][:, a, block(g)], ident[:])
 
         def gather(n, a):
             nc.vector.tensor_copy(trig[n][:, a, :], tabs[n][a][:].indirect(pos[:]))
@@ -99,17 +100,18 @@ def tile_attend_freshrope_pl_kernel(tc, emb_words, emb_scales, wk, cosn, sinn, o
             still, moving = (e, w) if w_moves else (w, e)
             nc.tensor.matmul_mx(out=out, lhsT=still[0], lhsT_scale=still[1], rhs=moving[0], rhs_scale=moving[1], start=True, stop=True)
 
-        b_turned = sb.tile([P, PACK, 2, P], F32, name="b_turned")
-        for g in range(2):
+        b_turned = [sb.tile([P, PACK, P], F32, name="b_turned%d" % g, tag="b_turned%d" % g) for g in range(2)]
+        for g in (1, 0):
             bank = ps.tile([P, PACK, P], F32, name="bt%d" % g, tag="block%d" % g)
             product(bank[:].rearrange("p t m -> p (t m)"), slice(0, D), block(g), True)
-            nc.scalar.copy(b_turned[:, :, g, :], bank[:])
+            nc.scalar.copy(b_turned[g][:], bank[:])
         banks = [ps.tile([P, 2, HALF], F32, name="bank%d" % a) for a in range(2)]
         b_plain = sb.tile([P, 2, 2, HALF], F32, name="b_plain")
-        for a in range(2):
+        for a in (1, 0):
             for e in range(2):
                 product(banks[a][:, e, :], block(2 * a + e), slots(1), False)
-            nc.scalar.copy(b_plain[:, a], banks[a][:])
+        nc.scalar.copy(b_plain[:, 1], banks[1][:])
+        nc.scalar.copy(b_plain[:, 0, :, :GP_SLOTS], banks[0][:, :, :GP_SLOTS])
 
         gather(1, 0)
         for h in (1, 0):
@@ -117,9 +119,9 @@ def tile_attend_freshrope_pl_kernel(tc, emb_words, emb_scales, wk, cosn, sinn, o
         turn(1, 1)
 
         ys = sb.tile([P, PACK, I], F32, name="ys")
-        terms = sb.tile([P, 7, 2, HALF], F32, name="terms", tag="tab11")
-        cos_plain = terms[:, 4:6]
-        sin_plain = [terms[:, 6], ys[:, 0:2, slots(1)]]
+        terms = sb.tile([P, 6, 2, HALF], F32, name="terms", tag="tab11")
+        cos_plain = terms[:, 4]
+        sin_plain = [terms[:, 5], ys[:, 0:2, slots(1)]]
         out_view = out_0.rearrange("(p t) i -> p t i", t=PACK)
         words = out_1[0].rearrange("p n t -> p (n t)").bitcast(I32)
 
@@ -135,42 +137,43 @@ def tile_attend_freshrope_pl_kernel(tc, emb_words, emb_scales, wk, cosn, sinn, o
 
         sums = [ps.tile([P, PACK, P], F32, name="sum%d" % g, tag="block%d" % g) for g in range(2)]
 
-        def terms_turned(a):
-            b = b_turned[:, 2 * a : 2 * a + 2].rearrange("p e g m -> p e (g m)")
-            cos, sin = (turned[n][a][:].rearrange("p g m -> p (g m)") for n in range(2))
-            cos_term, sin_term = terms[:, 2 * a], terms[:, 2 * a + 1]
-            nc.vector.tensor_tensor(cos_term, cos.unsqueeze(1).to_broadcast([P, 2, HALF]), b, MULT)
-            nc.vector.scalar_tensor_tensor(sin_term[:, 0, :], sin, -1.0, b[:, 1, :], MULT, MULT)
-            nc.vector.tensor_tensor(sin_term[:, 1, :], sin, b[:, 0, :], MULT)
-            for n, term in enumerate((cos_term, sin_term)):
-                for g in (1, 0):
-                    for e in range(2):
-                        nc.tensor.matmul(sums[g][:, 2 * a + e, :], term[:, e, block(g)], ident[:], is_transpose=True,
-                                         start=(n == 0 and e == 0), stop=(n == 1 and e == 1))
+        def terms_turned(g):
+            b = b_turned[g][:].rearrange("p (a e) m -> p a e m", e=2)
+            cos, sin = (turned[n][:, g] for n in range(2))
+            cos_term, sin_term = (terms[:, 2 * g + n].rearrange("p a (e m) -> p a e m", e=2) for n in range(2))
+            nc.vector.tensor_tensor(cos_term, cos.unsqueeze(2).to_broadcast([P, 2, 2, P]), b, MULT)
+            nc.vector.scalar_tensor_tensor(sin_term[:, :, 0, :], sin, -1.0, b[:, :, 1, :], MULT, MULT)
+            nc.vector.tensor_tensor(sin_term[:, :, 1, :], sin, b[:, :, 0, :], MULT)
+            steps = [(cos_term, a, e) for a in range(2) for e in range(2)] + [(sin_term, a, e) for e in range(2) for a in range(2)]
+            for n, (term, a, e) in enumerate(steps):
+                nc.tensor.matmul(sums[g][:, 2 * a + e, :], term[:, a, e, :], ident[:], is_transpose=True, start=(n == 0), stop=(n == len(steps) - 1))
 
-        def copy_out(a):
-            for g in (1, 0):
-                nc.scalar.copy(ys[:, 2 * a : 2 * a + 2, block(g)], sums[g][:, 2 * a : 2 * a + 2, :])
-            store(a, 0)
+        def copy_out(g):
+            nc.scalar.copy(ys[:, :, block(g)], sums[g][:])
+            nc.scalar.dma_start(out_view[:, :, block(g)], ys[:, :, block(g)])
+            nc.scalar.copy(y_bf[:, block(g), :], sums[g][:].rearrange("p t i -> p i t"))
 
         y_bf = sb.tile([P, I, PACK], BF16, name="y_bf", align_bytes=64)
         y_scales = sb.tile([P, I], U8, name="y_scales", align_bytes=64)
 
-        nc.gpsimd.tensor_tensor(cos_plain, b_plain[:], trig[0][:, :, slots(1)].unsqueeze(2).to_broadcast([P, 2, 2, HALF]), MULT)
+        cos0 = trig[0][:, 0, slots(1)].unsqueeze(1).to_broadcast([P, 2, HALF])
+        nc.gpsimd.tensor_tensor(cos_plain, b_plain[:, 1], trig[0][:, 1, slots(1)].unsqueeze(1).to_broadcast([P, 2, HALF]), MULT)
         sin_term_plain(1, 0)
-        nc.gpsimd.tensor_tensor(ys[:, 2, slots(1)], cos_plain[:, 1, 0], sin_plain[1][:, 0], ADD)
-        terms_turned(0)
-        copy_out(0)
+        sin_term_plain(1, 1)
+        nc.gpsimd.tensor_tensor(ys[:, 2:4, slots(1)], cos_plain, sin_plain[1], ADD)
+        store(1, 1)
         terms_turned(1)
         copy_out(1)
-        for g in (1, 0):
-            nc.scalar.copy(y_bf[:, block(g), :], sums[g][:].rearrange("p t i -> p i t"))
-        sin_term_plain(1, 1)
+        cos_last = sb.tile([P, 2, HALF], F32, name="cos_last", tag="b_turned1")
+        nc.gpsimd.tensor_tensor(cos_last[:, :, :GP_SLOTS], b_plain[:, 0, :, :GP_SLOTS], cos0[:, :, :GP_SLOTS], MULT)
+        terms_turned(0)
+        copy_out(0)
+        nc.vector.tensor_tensor(cos_last[:, :, GP_SLOTS:], banks[0][:, :, GP_SLOTS:], cos0[:, :, GP_SLOTS:], MULT)
         sin_term_plain(0, 0)
         sin_term_plain(0, 1)
 
         def add_plain(a, lo, hi):
-            nc.vector.tensor_tensor(ys[:, 2 * a : 2 * a + 2, HALF + lo : HALF + hi], cos_plain[:, a, :, lo:hi], sin_plain[a][:, :, lo:hi], ADD)
+            nc.vector.tensor_tensor(ys[:, 2 * a : 2 * a + 2, HALF + lo : HALF + hi], cos_last[:, :, lo:hi], sin_plain[a][:, :, lo:hi], ADD)
 
         def round_plain(g):
             nc.vector.tensor_copy(y_bf[:, block(g), :].rearrange("p (c i) t -> p c t i", i=4), ys[:, :, block(g)].rearrange("p t (c i) -> p c t i", i=4))
@@ -183,8 +186,6 @@ def tile_attend_freshrope_pl_kernel(tc, emb_words, emb_scales, wk, cosn, sinn, o
         def store_codes(cols):
             nc.sync.dma_start(words[:, cols], y_codes[:, cols].bitcast(I32))
 
-        nc.vector.tensor_tensor(ys[:, 3, slots(1)], cos_plain[:, 1, 1], sin_plain[1][:, 1], ADD)
-        store(1, 1)
         add_plain(0, 0, QUARTER)
         add_plain(0, QUARTER, HALF)
         store(0, 1)

@@ -119,7 +119,7 @@ def tile_attend_freshrope_pl_kernel(tc, emb_words, emb_scales, wk, cosn, sinn, o
         turn(1, 1)
 
         ys = sb.tile([P, PACK, I], F32, name="ys")
-        terms = sb.tile([P, 6, 2, HALF], F32, name="terms", tag="tab11")
+        terms = sb.tile([P, 7, 2, HALF], F32, name="terms", tag="tab11")
         cos_plain = terms[:, 4]
         sin_plain = [terms[:, 5], ys[:, 0:2, slots(1)]]
         out_view = out_0.rearrange("(p t) i -> p t i", t=PACK)
@@ -159,13 +159,13 @@ def tile_attend_freshrope_pl_kernel(tc, emb_words, emb_scales, wk, cosn, sinn, o
         cos0 = trig[0][:, 0, slots(1)].unsqueeze(1).to_broadcast([P, 2, HALF])
         nc.gpsimd.tensor_tensor(cos_plain, b_plain[:, 1], trig[0][:, 1, slots(1)].unsqueeze(1).to_broadcast([P, 2, HALF]), MULT)
         sin_term_plain(1, 0)
+        cos_last = terms[:, 6]
+        nc.gpsimd.tensor_tensor(cos_last[:, :, :GP_SLOTS], b_plain[:, 0, :, :GP_SLOTS], cos0[:, :, :GP_SLOTS], MULT)
+        terms_turned(1)
+        copy_out(1)
         sin_term_plain(1, 1)
         nc.gpsimd.tensor_tensor(ys[:, 2:4, slots(1)], cos_plain, sin_plain[1], ADD)
         store(1, 1)
-        terms_turned(1)
-        copy_out(1)
-        cos_last = sb.tile([P, 2, HALF], F32, name="cos_last", tag="b_turned1")
-        nc.gpsimd.tensor_tensor(cos_last[:, :, :GP_SLOTS], b_plain[:, 0, :, :GP_SLOTS], cos0[:, :, :GP_SLOTS], MULT)
         terms_turned(0)
         copy_out(0)
         nc.vector.tensor_tensor(cos_last[:, :, GP_SLOTS:], banks[0][:, :, GP_SLOTS:], cos0[:, :, GP_SLOTS:], MULT)

@@ -141,7 +141,8 @@ def tile_attend_freshrope_pl_kernel(tc, emb_words, emb_scales, wk, cosn, sinn, o
             b = b_turned[g][:].rearrange("p (a e) m -> p a e m", e=2)
             cos, sin = (turned[n][:, g] for n in range(2))
             cos_term, sin_term = (terms[:, 2 * g + n].rearrange("p a (e m) -> p a e m", e=2) for n in range(2))
-            nc.vector.tensor_tensor(cos_term, cos.unsqueeze(2).to_broadcast([P, 2, 2, P]), b, MULT)
+            for a in range(2):
+                nc.vector.tensor_tensor(cos_term[:, a], cos[:, a].unsqueeze(1).to_broadcast([P, 2, P]), b[:, a], MULT)
             nc.vector.scalar_tensor_tensor(sin_term[:, :, 0, :], sin, -1.0, b[:, :, 1, :], MULT, MULT)
             nc.vector.tensor_tensor(sin_term[:, :, 1, :], sin, b[:, :, 0, :], MULT)
             steps = [(cos_term, a, e) for a in range(2) for e in range(2)] + [(sin_term, a, e) for e in range(2) for a in range(2)]

@@ -1,7 +1,6 @@
 from contextlib import ExitStack
 
 import concourse.mybir as mybir
-from concourse.masks import make_identity
 
 K, T, I, D, U = 512, 2048, 512, 512, 1024
 FLOPS = 2 * K * D * I
@@ -16,14 +15,13 @@ U8 = mybir.dt.uint8
 FP8X4 = mybir.dt.float8_e4m3fn_x4
 MULT = mybir.AluOpType.mult
 ADD = mybir.AluOpType.add
-SUB = mybir.AluOpType.subtract
+COPY = mybir.ActivationFunctionType.Copy
 
 P = 128
 PACK = 4
 HALF = I // 2
-QUARTER = I // 4
 LIST_COLS = I // 16
-GP_SLOTS = 128
+COS, SIN = 0, 1
 
 
 def tile_attend_freshrope_pl_kernel(tc, emb_words, emb_scales, wk, cosn, sinn, offs, offs2, out_0, out_1, out_2):
@@ -37,48 +35,32 @@ def tile_attend_freshrope_pl_kernel(tc, emb_words, emb_scales, wk, cosn, sinn, o
         w_raw = sb.tile([P, PACK, D], F32, name="w_raw")
         e_pool = sb.tile([P, T], I32, name="e_pool", align_bytes=64)
         s_pool = sb.tile([P, T], U8, name="s_pool", align_bytes=64)
-        tabs = [[sb.tile([P, U], F32, name="tab%d%d" % (n, a), tag="tab%d%d" % (n, a)) for a in range(2)] for n in range(2)]
-        ident = sb.tile([P, P], F32, name="ident")
+        tables = [[sb.tile([P, U], F32, name="table%d%d" % (n, a)) for a in range(2)] for n in range(2)]
 
         def load_table(n, a):
-            nc.sync.dma_start(tabs[n][a][:], (cosn, sinn)[n].rearrange("(p t) u -> p t u", t=PACK)[:, 2 * a, :])
+            nc.sync.dma_start(tables[n][a][:], (cosn, sinn)[n].rearrange("(p t) u -> p t u", t=PACK)[:, 2 * a, :])
 
         nc.vector.memset(s_pool[:].bitcast(I32), 0)
-        make_identity(nc, ident[:])
-        load_table(0, 0)
         nc.sync.dma_start(pos[:], offs2)
+        nc.sync.dma_start(w_raw[:], wk.rearrange("(p j) d -> p j d", j=PACK))
         nc.sync.dma_start(tok[:], offs)
         for r in range(4):
             nc.sync.dma_start(s_pool[r:P:32, :].bitcast(I32), emb_scales[0].rearrange("(q r) n -> r q n", r=4)[r].bitcast(I32))
-        nc.sync.dma_start(w_raw[:], wk.rearrange("(p j) d -> p j d", j=PACK))
-        load_table(0, 1)
         nc.sync.dma_start(e_pool[:], emb_words[0].rearrange("p n t -> p (n t)").bitcast(I32))
-        load_table(1, 0)
-        load_table(1, 1)
+        for a in range(2):
+            for n in (COS, SIN):
+                load_table(n, a)
 
         def slots(h):
             return slice(h * HALF, (h + 1) * HALF)
 
-        def block(g):
-            return slice(g * P, (g + 1) * P)
-
         def entries(lst, h):
             return lst[:, h * LIST_COLS // 2 : (h + 1) * LIST_COLS // 2]
 
-        trig = [sb.tile([P, 2, I], F32, name="trig%d" % n) for n in range(2)]
-        turned = [ps.tile([P, 2, 2, P], F32, name="turned%d" % n) for n in range(2)]
+        trig = [[sb.tile([P, I], F32, name="trig%d%d" % (n, a)) for a in range(2)] for n in range(2)]
 
-        def turn(n, a):
-            for g in (1, 0):
-                nc.tensor.transpose(turned[n][:, g, a, :], trig[n][:, a, block(g)], ident[:])
-
-        def gather(n, a):
-            nc.vector.tensor_copy(trig[n][:, a, :], tabs[n][a][:].indirect(pos[:]))
-            turn(n, a)
-
-        gather(0, 0)
-        e_scales = sb.tile([P, I], U8, name="e_scales", align_bytes=64)
-        nc.vector.tensor_copy(e_scales[:], s_pool[:].indirect(tok[:]))
+        def gather(n, a, h):
+            nc.scalar.activation(trig[n][a][:, slots(h)], tables[n][a][:].indirect(entries(pos, h)), COPY)
 
         w_codes = sb.tile([P, D], U32, name="w_codes", align_bytes=64)
         w_scales = sb.tile([P, D], U8, name="w_scales", align_bytes=64)
@@ -89,114 +71,76 @@ def tile_attend_freshrope_pl_kernel(tc, emb_words, emb_scales, wk, cosn, sinn, o
             cols = slice(2 * P * a, 2 * P * (a + 1))
             nc.vector.quantize_mx(out=w_codes[:, cols].bitcast(FP8X4), scales=w_scales[:, cols], in_=w_bf[:].rearrange("p t m j -> p (t m j)"))
 
-        gather(0, 1)
+        e_scales = sb.tile([P, I], U8, name="e_scales", align_bytes=64)
+        nc.vector.tensor_copy(e_scales[:], s_pool[:].indirect(tok[:]))
         e_codes = sb.tile([P, I], U32, name="e_codes", align_bytes=64)
+        banks = [[ps.tile([P, 2, HALF], F32, name="bank%d%d" % (a, h)) for h in range(2)] for a in range(2)]
         for h in range(2):
             nc.vector.tensor_copy(e_codes[:, slots(h)], e_pool[:].bitcast(U32).indirect(entries(tok, h)))
-
-        def product(out, w_cols, e_cols, w_moves):
-            w = (w_codes[:, w_cols].bitcast(FP8X4), w_scales[:, w_cols])
-            e = (e_codes[:, e_cols].bitcast(FP8X4), e_scales[:, e_cols])
-            still, moving = (e, w) if w_moves else (w, e)
-            nc.tensor.matmul_mx(out=out, lhsT=still[0], lhsT_scale=still[1], rhs=moving[0], rhs_scale=moving[1], start=True, stop=True)
-
-        b_turned = [sb.tile([P, PACK, P], F32, name="b_turned%d" % g, tag="b_turned%d" % g) for g in range(2)]
-        for g in (1, 0):
-            bank = ps.tile([P, PACK, P], F32, name="bt%d" % g, tag="block%d" % g)
-            product(bank[:].rearrange("p t m -> p (t m)"), slice(0, D), block(g), True)
-            nc.scalar.copy(b_turned[g][:], bank[:])
-        banks = [ps.tile([P, 2, HALF], F32, name="bank%d" % a) for a in range(2)]
-        b_plain = sb.tile([P, 2, 2, HALF], F32, name="b_plain")
-        for a in (1, 0):
-            for e in range(2):
-                product(banks[a][:, e, :], block(2 * a + e), slots(1), False)
-        nc.scalar.copy(b_plain[:, 1], banks[1][:])
-        nc.scalar.copy(b_plain[:, 0, :, :GP_SLOTS], banks[0][:, :, :GP_SLOTS])
-
-        gather(1, 0)
-        for h in (1, 0):
-            nc.vector.tensor_copy(trig[1][:, 1, slots(h)], tabs[1][1][:].indirect(entries(pos, h)))
-        turn(1, 1)
+        for a in range(2):
+            for h in range(2):
+                for e in range(2):
+                    cols = slice((2 * a + e) * P, (2 * a + e + 1) * P)
+                    nc.tensor.matmul_mx(
+                        out=banks[a][h][:, e, :],
+                        lhsT=w_codes[:, cols].bitcast(FP8X4),
+                        lhsT_scale=w_scales[:, cols],
+                        rhs=e_codes[:, slots(h)].bitcast(FP8X4),
+                        rhs_scale=e_scales[:, slots(h)],
+                        start=True,
+                        stop=True,
+                    )
 
         ys = sb.tile([P, PACK, I], F32, name="ys")
-        terms = sb.tile([P, 7, 2, HALF], F32, name="terms", tag="tab11")
-        cos_plain = terms[:, 4]
-        sin_plain = [terms[:, 5], ys[:, 0:2, slots(1)]]
+        terms = [[sb.tile([P, 2, I], F32, name="term%d%d" % (n, a)) for a in range(2)] for n in range(2)]
         out_view = out_0.rearrange("(p t) i -> p t i", t=PACK)
         words = out_1[0].rearrange("p n t -> p (n t)").bitcast(I32)
 
-        def store(a, h):
-            nc.sync.dma_start(out_view[:, 2 * a : 2 * a + 2, slots(h)], ys[:, 2 * a : 2 * a + 2, slots(h)])
+        def cos_term(a, h):
+            cos = trig[COS][a][:, slots(h)].unsqueeze(1).to_broadcast([P, 2, HALF])
+            nc.vector.tensor_tensor(terms[COS][a][:, :, slots(h)], banks[a][h][:], cos, MULT)
 
-        def sin_term_plain(a, e):
-            sin = trig[1][:, a, slots(1)]
-            if e == 0:
-                nc.vector.scalar_tensor_tensor(sin_plain[a][:, 0, :], banks[a][:, 1, :], -1.0, sin, MULT, MULT)
-            else:
-                nc.vector.tensor_tensor(sin_plain[a][:, 1, :], banks[a][:, 0, :], sin, MULT)
+        def sin_term(a, h):
+            sin = trig[SIN][a][:, slots(h)]
+            nc.vector.scalar_tensor_tensor(terms[SIN][a][:, 0, slots(h)], banks[a][h][:, 1, :], -1.0, sin, MULT, MULT)
+            nc.vector.tensor_tensor(terms[SIN][a][:, 1, slots(h)], banks[a][h][:, 0, :], sin, MULT)
 
-        sums = [ps.tile([P, PACK, P], F32, name="sum%d" % g, tag="block%d" % g) for g in range(2)]
-
-        def terms_turned(g):
-            b = b_turned[g][:].rearrange("p (a e) m -> p a e m", e=2)
-            cos, sin = (turned[n][:, g] for n in range(2))
-            cos_term, sin_term = (terms[:, 2 * g + n].rearrange("p a (e m) -> p a e m", e=2) for n in range(2))
-            for a in range(2):
-                nc.vector.tensor_tensor(cos_term[:, a], cos[:, a].unsqueeze(1).to_broadcast([P, 2, P]), b[:, a], MULT)
-            nc.vector.scalar_tensor_tensor(sin_term[:, :, 0, :], sin, -1.0, b[:, :, 1, :], MULT, MULT)
-            nc.vector.tensor_tensor(sin_term[:, :, 1, :], sin, b[:, :, 0, :], MULT)
-            steps = [(cos_term, a, e) for a in range(2) for e in range(2)] + [(sin_term, a, e) for e in range(2) for a in range(2)]
-            for n, (term, a, e) in enumerate(steps):
-                nc.tensor.matmul(sums[g][:, 2 * a + e, :], term[:, a, e, :], ident[:], is_transpose=True, start=(n == 0), stop=(n == len(steps) - 1))
-
-        def copy_out(g):
-            nc.scalar.copy(ys[:, :, block(g)], sums[g][:])
-            nc.scalar.dma_start(out_view[:, :, block(g)], ys[:, :, block(g)])
-            nc.scalar.copy(y_bf[:, block(g), :], sums[g][:].rearrange("p t i -> p i t"))
+        def add_and_store(engine, a, h):
+            y = ys[:, 2 * a : 2 * a + 2, slots(h)]
+            engine.tensor_tensor(y, terms[COS][a][:, :, slots(h)], terms[SIN][a][:, :, slots(h)], ADD)
+            nc.sync.dma_start(out_view[:, 2 * a : 2 * a + 2, slots(h)], y)
 
         y_bf = sb.tile([P, I, PACK], BF16, name="y_bf", align_bytes=64)
+        y_codes = sb.tile([P, I], U32, name="y_codes", align_bytes=64)
         y_scales = sb.tile([P, I], U8, name="y_scales", align_bytes=64)
 
-        cos0 = trig[0][:, 0, slots(1)].unsqueeze(1).to_broadcast([P, 2, HALF])
-        nc.gpsimd.tensor_tensor(cos_plain, b_plain[:, 1], trig[0][:, 1, slots(1)].unsqueeze(1).to_broadcast([P, 2, HALF]), MULT)
-        sin_term_plain(1, 0)
-        cos_last = terms[:, 6]
-        nc.gpsimd.tensor_tensor(cos_last[:, :, :GP_SLOTS], b_plain[:, 0, :, :GP_SLOTS], cos0[:, :, :GP_SLOTS], MULT)
-        terms_turned(1)
-        copy_out(1)
-        sin_term_plain(1, 1)
-        nc.gpsimd.tensor_tensor(ys[:, 2:4, slots(1)], cos_plain, sin_plain[1], ADD)
-        store(1, 1)
-        terms_turned(0)
-        copy_out(0)
-        nc.vector.tensor_tensor(cos_last[:, :, GP_SLOTS:], banks[0][:, :, GP_SLOTS:], cos0[:, :, GP_SLOTS:], MULT)
-        sin_term_plain(0, 0)
-        sin_term_plain(0, 1)
+        def round_y(copy, h):
+            copy(y_bf[:, slots(h), :].rearrange("p (c i) t -> p c t i", i=4), ys[:, :, slots(h)].rearrange("p t (c i) -> p c t i", i=4))
 
-        def add_plain(a, lo, hi):
-            nc.vector.tensor_tensor(ys[:, 2 * a : 2 * a + 2, HALF + lo : HALF + hi], cos_last[:, :, lo:hi], sin_plain[a][:, :, lo:hi], ADD)
+        def quantize_and_store(h):
+            nc.vector.quantize_mx(
+                out=y_codes[:, slots(h)].bitcast(FP8X4), scales=y_scales[:, slots(h)], in_=y_bf[:, slots(h), :].rearrange("p i t -> p (i t)")
+            )
+            nc.sync.dma_start(words[:, slots(h)], y_codes[:, slots(h)].bitcast(I32))
 
-        def round_plain(g):
-            nc.vector.tensor_copy(y_bf[:, block(g), :].rearrange("p (c i) t -> p c t i", i=4), ys[:, :, block(g)].rearrange("p t (c i) -> p c t i", i=4))
-
-        y_codes = sb.tile([P, I], U32, name="y_codes", align_bytes=64)
-
-        def quantize(cols):
-            nc.vector.quantize_mx(out=y_codes[:, cols].bitcast(FP8X4), scales=y_scales[:, cols], in_=y_bf[:, cols, :].rearrange("p i t -> p (i t)"))
-
-        def store_codes(cols):
-            nc.sync.dma_start(words[:, cols], y_codes[:, cols].bitcast(I32))
-
-        add_plain(0, 0, QUARTER)
-        add_plain(0, QUARTER, HALF)
-        store(0, 1)
-        round_plain(2)
-        round_plain(3)
-        quantize(block(1))
-        quantize(slots(1))
-        store_codes(slots(1))
-        quantize(block(0))
-        store_codes(slots(0))
+        for a in range(2):
+            for n in (COS, SIN):
+                for h in range(2):
+                    gather(n, a, h)
+        for h in range(2):
+            cos_term(0, h)
+        for h in range(2):
+            sin_term(0, h)
+            add_and_store(nc.gpsimd, 0, h)
+        for h in range(2):
+            cos_term(1, h)
+        for h in range(2):
+            sin_term(1, h)
+            add_and_store(nc.vector, 1, h)
+        round_y(nc.scalar.copy, 0)
+        round_y(nc.vector.tensor_copy, 1)
+        for h in range(2):
+            quantize_and_store(h)
         for q in range(4):
             queue = nc.sync if q < 2 else nc.scalar
             queue.dma_start(out_2[0, 4 * q : 4 * q + 4, :].bitcast(I32), y_scales[32 * q : 32 * q + 4, :].bitcast(I32))

@@ -20,6 +20,7 @@ COPY = mybir.ActivationFunctionType.Copy
 P = 128
 PACK = 4
 HALF = I // 2
+QUARTER = I // 4
 LIST_COLS = I // 16
 COS, SIN = 0, 1
 
@@ -96,31 +97,41 @@ def tile_attend_freshrope_pl_kernel(tc, emb_words, emb_scales, wk, cosn, sinn, o
         out_view = out_0.rearrange("(p t) i -> p t i", t=PACK)
         words = out_1[0].rearrange("p n t -> p (n t)").bitcast(I32)
 
-        def cos_term(a, h):
-            cos = trig[COS][a][:, slots(h)].unsqueeze(1).to_broadcast([P, 2, HALF])
-            nc.vector.tensor_tensor(terms[COS][a][:, :, slots(h)], banks[a][h][:], cos, MULT)
+        def span(lo, hi):
+            return slice(lo * QUARTER, hi * QUARTER)
 
-        def sin_term(a, h):
-            sin = trig[SIN][a][:, slots(h)]
-            nc.vector.scalar_tensor_tensor(terms[SIN][a][:, 0, slots(h)], banks[a][h][:, 1, :], -1.0, sin, MULT, MULT)
-            nc.vector.tensor_tensor(terms[SIN][a][:, 1, slots(h)], banks[a][h][:, 0, :], sin, MULT)
+        def bank(a, lo, hi):
+            return banks[a][lo // 2][:, :, span(lo % 2, lo % 2 + hi - lo)]
 
-        def add_and_store(engine, a, h):
-            y = ys[:, 2 * a : 2 * a + 2, slots(h)]
-            engine.tensor_tensor(y, terms[COS][a][:, :, slots(h)], terms[SIN][a][:, :, slots(h)], ADD)
-            nc.sync.dma_start(out_view[:, 2 * a : 2 * a + 2, slots(h)], y)
+        def cos_term(a, lo, hi):
+            cos = trig[COS][a][:, span(lo, hi)].unsqueeze(1).to_broadcast([P, 2, (hi - lo) * QUARTER])
+            nc.vector.tensor_tensor(terms[COS][a][:, :, span(lo, hi)], bank(a, lo, hi), cos, MULT)
 
-        y_bf = sb.tile([P, I, PACK], BF16, name="y_bf", align_bytes=64)
+        def sin_term(a, lo, hi):
+            sin = trig[SIN][a][:, span(lo, hi)]
+            b = bank(a, lo, hi)
+            nc.vector.scalar_tensor_tensor(terms[SIN][a][:, 0, span(lo, hi)], b[:, 1, :], -1.0, sin, MULT, MULT)
+            nc.vector.tensor_tensor(terms[SIN][a][:, 1, span(lo, hi)], b[:, 0, :], sin, MULT)
+
+        def add(engine, a, lo, hi):
+            engine.tensor_tensor(ys[:, 2 * a : 2 * a + 2, span(lo, hi)], terms[COS][a][:, :, span(lo, hi)], terms[SIN][a][:, :, span(lo, hi)], ADD)
+
+        def store(a, h):
+            nc.sync.dma_start(out_view[:, 2 * a : 2 * a + 2, slots(h)], ys[:, 2 * a : 2 * a + 2, slots(h)])
+
+        y_bf = [sb.tile([P, QUARTER, PACK], BF16, name="y_bf%d" % q, align_bytes=64) for q in range(4)]
         y_codes = sb.tile([P, I], U32, name="y_codes", align_bytes=64)
         y_scales = sb.tile([P, I], U8, name="y_scales", align_bytes=64)
 
-        def round_y(copy, h):
-            copy(y_bf[:, slots(h), :].rearrange("p (c i) t -> p c t i", i=4), ys[:, :, slots(h)].rearrange("p t (c i) -> p c t i", i=4))
+        def round_y(copy, q):
+            cols = span(q, q + 1)
+            copy(y_bf[q][:].rearrange("p (c i) t -> p c t i", i=4), ys[:, :, cols].rearrange("p t (c i) -> p c t i", i=4))
 
-        def quantize_and_store(h):
-            nc.vector.quantize_mx(
-                out=y_codes[:, slots(h)].bitcast(FP8X4), scales=y_scales[:, slots(h)], in_=y_bf[:, slots(h), :].rearrange("p i t -> p (i t)")
-            )
+        def quantize(q):
+            cols = span(q, q + 1)
+            nc.vector.quantize_mx(out=y_codes[:, cols].bitcast(FP8X4), scales=y_scales[:, cols], in_=y_bf[q][:].rearrange("p i t -> p (i t)"))
+
+        def store_codes(h):
             nc.sync.dma_start(words[:, slots(h)], y_codes[:, slots(h)].bitcast(I32))
 
         for a in range(2):
@@ -128,19 +139,29 @@ def tile_attend_freshrope_pl_kernel(tc, emb_words, emb_scales, wk, cosn, sinn, o
                 for h in range(2):
                     gather(n, a, h)
         for h in range(2):
-            cos_term(0, h)
+            cos_term(0, 2 * h, 2 * h + 2)
         for h in range(2):
-            sin_term(0, h)
-            add_and_store(nc.gpsimd, 0, h)
+            sin_term(0, 2 * h, 2 * h + 2)
+            add(nc.gpsimd, 0, 2 * h, 2 * h + 2)
+            store(0, h)
         for h in range(2):
-            cos_term(1, h)
-        for h in range(2):
-            sin_term(1, h)
-            add_and_store(nc.vector, 1, h)
-        round_y(nc.scalar.copy, 0)
-        round_y(nc.vector.tensor_copy, 1)
-        for h in range(2):
-            quantize_and_store(h)
+            cos_term(1, 2 * h, 2 * h + 2)
+        sin_term(1, 0, 1)
+        for q in range(4):
+            if q < 3:
+                sin_term(1, q + 1, q + 2)
+            add(nc.vector, 1, q, q + 1)
+            if q % 2 == 1:
+                store(1, q // 2)
+            if q < 3:
+                round_y(nc.scalar.copy, q)
+        quantize(0)
+        quantize(1)
+        store_codes(0)
+        round_y(nc.vector.tensor_copy, 3)
+        quantize(2)
+        quantize(3)
+        store_codes(1)
         for q in range(4):
             queue = nc.sync if q < 2 else nc.scalar
             queue.dma_start(out_2[0, 4 * q : 4 * q + 4, :].bitcast(I32), y_scales[32 * q : 32 * q + 4, :].bitcast(I32))

@@ -22,6 +22,7 @@ PACK = 4
 HALF = I // 2
 QUARTER = I // 4
 LIST_COLS = I // 16
+W_SPLIT = 96
 COS, SIN = 0, 1
 
 
@@ -66,13 +67,19 @@ def tile_attend_freshrope_pl_kernel(tc, emb_words, emb_scales, wk, cosn, sinn, o
         w_codes = sb.tile([P, D], U32, name="w_codes", align_bytes=64)
         w_scales = sb.tile([P, D], U8, name="w_scales", align_bytes=64)
         w_view = w_raw[:].rearrange("p j (m t) -> p m t j", t=PACK)
-        for a in range(2):
-            w_bf = sb.tile([P, 2, P, PACK], BF16, name="w_bf%d" % a, align_bytes=64)
-            (nc.vector.tensor_copy, nc.scalar.copy)[a](w_bf[:].rearrange("p t m j -> p m t j"), w_view[:, :, 2 * a : 2 * a + 2, :])
-            cols = slice(2 * P * a, 2 * P * (a + 1))
-            nc.vector.quantize_mx(out=w_codes[:, cols].bitcast(FP8X4), scales=w_scales[:, cols], in_=w_bf[:].rearrange("p t m j -> p (t m j)"))
+        w_bf = [sb.tile([P, 2, P, PACK], BF16, name="w_bf%d" % a, tag="w_bf%d" % a, align_bytes=64) for a in range(2)]
 
-        e_scales = sb.tile([P, I], U8, name="e_scales", align_bytes=64)
+        def round_w(copy, a, lo, hi):
+            copy(w_bf[a][:, :, lo:hi, :].rearrange("p t m j -> p m t j"), w_view[:, lo:hi, 2 * a : 2 * a + 2, :])
+
+        round_w(nc.scalar.copy, 1, 0, W_SPLIT)
+        round_w(nc.vector.tensor_copy, 0, 0, P)
+        round_w(nc.vector.tensor_copy, 1, W_SPLIT, P)
+        for a in range(2):
+            cols = slice(2 * P * a, 2 * P * (a + 1))
+            nc.vector.quantize_mx(out=w_codes[:, cols].bitcast(FP8X4), scales=w_scales[:, cols], in_=w_bf[a][:].rearrange("p t m j -> p (t m j)"))
+
+        e_scales = sb.tile([P, I], U8, name="e_scales", tag="w_bf1", align_bytes=64)
         nc.vector.tensor_copy(e_scales[:], s_pool[:].indirect(tok[:]))
         e_codes = sb.tile([P, I], U32, name="e_codes", align_bytes=64)
         banks = [[ps.tile([P, 2, HALF], F32, name="bank%d%d" % (a, h)) for h in range(2)] for a in range(2)]
@@ -140,16 +147,17 @@ def tile_attend_freshrope_pl_kernel(tc, emb_words, emb_scales, wk, cosn, sinn, o
                     gather(n, a, h)
         for h in range(2):
             cos_term(0, 2 * h, 2 * h + 2)
-        for h in range(2):
-            sin_term(0, 2 * h, 2 * h + 2)
-            add(nc.gpsimd, 0, 2 * h, 2 * h + 2)
-            store(0, h)
+        for lo, hi in ((0, 1), (1, 2), (2, 4)):
+            sin_term(0, lo, hi)
+            add(nc.gpsimd, 0, lo, hi)
+            if hi % 2 == 0:
+                store(0, hi // 2 - 1)
         for h in range(2):
             cos_term(1, 2 * h, 2 * h + 2)
-        sin_term(1, 0, 1)
+        sin_term(1, 0, 2)
         for q in range(4):
-            if q < 3:
-                sin_term(1, q + 1, q + 2)
+            if q < 2:
+                sin_term(1, q + 2, q + 3)
             add(nc.vector, 1, q, q + 1)
             if q % 2 == 1:
                 store(1, q // 2)

@@ -37,15 +37,15 @@ def tile_attend_freshrope_pl_kernel(tc, emb_words, emb_scales, wk, cosn, sinn, o
         w_raw = sb.tile([P, PACK, D], F32, name="w_raw")
         e_pool = sb.tile([P, T], I32, name="e_pool", align_bytes=64)
         s_pool = sb.tile([P, T], U8, name="s_pool", align_bytes=64)
-        tables = [[sb.tile([P, U], F32, name="table%d%d" % (n, a)) for a in range(2)] for n in range(2)]
+        tables = [[sb.tile([P, U], F32, name="table%d%d" % (n, a), tag="table%d%d" % (n, a), align_bytes=64) for a in range(2)] for n in range(2)]
 
         def load_table(n, a):
             nc.sync.dma_start(tables[n][a][:], (cosn, sinn)[n].rearrange("(p t) u -> p t u", t=PACK)[:, 2 * a, :])
 
         nc.vector.memset(s_pool[:].bitcast(I32), 0)
-        nc.sync.dma_start(pos[:], offs2)
         nc.sync.dma_start(w_raw[:], wk.rearrange("(p j) d -> p j d", j=PACK))
         nc.sync.dma_start(tok[:], offs)
+        nc.sync.dma_start(pos[:], offs2)
         for r in range(4):
             nc.sync.dma_start(s_pool[r:P:32, :].bitcast(I32), emb_scales[0].rearrange("(q r) n -> r q n", r=4)[r].bitcast(I32))
         nc.sync.dma_start(e_pool[:], emb_words[0].rearrange("p n t -> p (n t)").bitcast(I32))
@@ -61,8 +61,14 @@ def tile_attend_freshrope_pl_kernel(tc, emb_words, emb_scales, wk, cosn, sinn, o
 
         trig = [[sb.tile([P, I], F32, name="trig%d%d" % (n, a)) for a in range(2)] for n in range(2)]
 
-        def gather(n, a, h):
-            nc.scalar.activation(trig[n][a][:, slots(h)], tables[n][a][:].indirect(entries(pos, h)), COPY)
+        def span(lo, hi):
+            return slice(lo * QUARTER, hi * QUARTER)
+
+        def looked_up(n, a, lo, hi):
+            return tables[n][a][:].indirect(pos[:, lo * LIST_COLS // 4 : hi * LIST_COLS // 4])
+
+        def gather(n, a, lo, hi):
+            nc.scalar.activation(trig[n][a][:, span(lo, hi)], looked_up(n, a, lo, hi), COPY)
 
         w_codes = sb.tile([P, D], U32, name="w_codes", align_bytes=64)
         w_scales = sb.tile([P, D], U8, name="w_scales", align_bytes=64)
@@ -104,9 +110,6 @@ def tile_attend_freshrope_pl_kernel(tc, emb_words, emb_scales, wk, cosn, sinn, o
         out_view = out_0.rearrange("(p t) i -> p t i", t=PACK)
         words = out_1[0].rearrange("p n t -> p (n t)").bitcast(I32)
 
-        def span(lo, hi):
-            return slice(lo * QUARTER, hi * QUARTER)
-
         def bank(a, lo, hi):
             return banks[a][lo // 2][:, :, span(lo % 2, lo % 2 + hi - lo)]
 
@@ -126,25 +129,33 @@ def tile_attend_freshrope_pl_kernel(tc, emb_words, emb_scales, wk, cosn, sinn, o
         def store(a, h):
             nc.sync.dma_start(out_view[:, 2 * a : 2 * a + 2, slots(h)], ys[:, 2 * a : 2 * a + 2, slots(h)])
 
-        y_bf = [sb.tile([P, QUARTER, PACK], BF16, name="y_bf%d" % q, align_bytes=64) for q in range(4)]
+        y_halves = [sb.tile([P, HALF, PACK], BF16, name="y_bf%d" % h, tag=("table11", "y_bf1")[h], align_bytes=64) for h in range(2)]
+        y_bf = [y_halves[q // 2][:, span(q % 2, q % 2 + 1), :] for q in range(4)]
         y_codes = sb.tile([P, I], U32, name="y_codes", align_bytes=64)
         y_scales = sb.tile([P, I], U8, name="y_scales", align_bytes=64)
 
         def round_y(copy, q):
             cols = span(q, q + 1)
-            copy(y_bf[q][:].rearrange("p (c i) t -> p c t i", i=4), ys[:, :, cols].rearrange("p t (c i) -> p c t i", i=4))
+            copy(y_bf[q].rearrange("p (c i) t -> p c t i", i=4), ys[:, :, cols].rearrange("p t (c i) -> p c t i", i=4))
+
+        def round_pair(copy, q, a):
+            copy(y_bf[q][:, :, 2 * a : 2 * a + 2], ys[:, 2 * a : 2 * a + 2, span(q, q + 1)].rearrange("p t i -> p i t"))
 
         def quantize(q):
             cols = span(q, q + 1)
-            nc.vector.quantize_mx(out=y_codes[:, cols].bitcast(FP8X4), scales=y_scales[:, cols], in_=y_bf[q][:].rearrange("p i t -> p (i t)"))
+            nc.vector.quantize_mx(out=y_codes[:, cols].bitcast(FP8X4), scales=y_scales[:, cols], in_=y_bf[q].rearrange("p i t -> p (i t)"))
 
         def store_codes(h):
             nc.sync.dma_start(words[:, slots(h)], y_codes[:, slots(h)].bitcast(I32))
 
-        for a in range(2):
-            for n in (COS, SIN):
-                for h in range(2):
-                    gather(n, a, h)
+        nc.vector.tensor_copy(trig[COS][0][:, span(0, 1)], looked_up(COS, 0, 0, 1))
+        gather(COS, 0, 1, 2)
+        gather(COS, 0, 2, 4)
+        for n, a in ((SIN, 0), (COS, 1)):
+            for h in range(2):
+                gather(n, a, 2 * h, 2 * h + 2)
+        for h in (1, 0):
+            gather(SIN, 1, 2 * h, 2 * h + 2)
         for h in range(2):
             cos_term(0, 2 * h, 2 * h + 2)
         for lo, hi in ((0, 1), (1, 2), (2, 4)):
@@ -154,22 +165,26 @@ def tile_attend_freshrope_pl_kernel(tc, emb_words, emb_scales, wk, cosn, sinn, o
                 store(0, hi // 2 - 1)
         for h in range(2):
             cos_term(1, 2 * h, 2 * h + 2)
-        sin_term(1, 0, 2)
-        for q in range(4):
-            if q < 2:
-                sin_term(1, q + 2, q + 3)
-            add(nc.vector, 1, q, q + 1)
-            if q % 2 == 1:
-                store(1, q // 2)
-            if q < 3:
-                round_y(nc.scalar.copy, q)
+        nc.scalar.copy(y_halves[0][:, :, 0:2], ys[:, 0:2, slots(0)].rearrange("p t i -> p i t"))
+        sin_term(1, 2, 4)
+        sin_term(1, 0, 1)
+        add(nc.vector, 1, 2, 3)
+        round_y(nc.scalar.copy, 2)
+        sin_term(1, 1, 2)
+        add(nc.vector, 1, 3, 4)
+        store(1, 1)
+        round_y(nc.scalar.copy, 3)
+        add(nc.vector, 1, 0, 1)
+        round_pair(nc.scalar.copy, 0, 1)
+        add(nc.vector, 1, 1, 2)
+        store(1, 0)
+        quantize(2)
+        round_pair(nc.vector.tensor_copy, 1, 1)
+        quantize(3)
+        store_codes(1)
         quantize(0)
         quantize(1)
         store_codes(0)
-        round_y(nc.vector.tensor_copy, 3)
-        quantize(2)
-        quantize(3)
-        store_codes(1)
         for q in range(4):
             queue = nc.sync if q < 2 else nc.scalar
             queue.dma_start(out_2[0, 4 * q : 4 * q + 4, :].bitcast(I32), y_scales[32 * q : 32 * q + 4, :].bitcast(I32))

@@ -67,8 +67,15 @@ def tile_attend_freshrope_pl_kernel(tc, emb_words, emb_scales, wk, cosn, sinn, o
         def looked_up(n, a, lo, hi):
             return tables[n][a][:].indirect(pos[:, lo * LIST_COLS // 4 : hi * LIST_COLS // 4])
 
+        terms = [[sb.tile([P, 2, I], F32, name="term%d%d" % (n, a)) for a in range(2)] for n in range(2)]
+
+        def gathered(n, a, lo, hi):
+            if (n, a) == (SIN, 0) and lo < 2:
+                return terms[COS][0][:, lo, span(3, 4)]
+            return trig[n][a][:, span(lo, hi)]
+
         def gather(n, a, lo, hi):
-            nc.scalar.activation(trig[n][a][:, span(lo, hi)], looked_up(n, a, lo, hi), COPY)
+            nc.scalar.activation(gathered(n, a, lo, hi), looked_up(n, a, lo, hi), COPY)
 
         w_codes = sb.tile([P, D], U32, name="w_codes", align_bytes=64)
         w_scales = sb.tile([P, D], U8, name="w_scales", align_bytes=64)
@@ -106,7 +113,6 @@ def tile_attend_freshrope_pl_kernel(tc, emb_words, emb_scales, wk, cosn, sinn, o
                     )
 
         ys = sb.tile([P, PACK, I], F32, name="ys")
-        terms = [[sb.tile([P, 2, I], F32, name="term%d%d" % (n, a)) for a in range(2)] for n in range(2)]
         out_view = out_0.rearrange("(p t) i -> p t i", t=PACK)
         words = out_1[0].rearrange("p n t -> p (n t)").bitcast(I32)
 
@@ -118,7 +124,7 @@ def tile_attend_freshrope_pl_kernel(tc, emb_words, emb_scales, wk, cosn, sinn, o
             nc.vector.tensor_tensor(terms[COS][a][:, :, span(lo, hi)], bank(a, lo, hi), cos, MULT)
 
         def sin_term(a, lo, hi):
-            sin = trig[SIN][a][:, span(lo, hi)]
+            sin = gathered(SIN, a, lo, hi)
             b = bank(a, lo, hi)
             nc.vector.scalar_tensor_tensor(terms[SIN][a][:, 0, span(lo, hi)], b[:, 1, :], -1.0, sin, MULT, MULT)
             nc.vector.tensor_tensor(terms[SIN][a][:, 1, span(lo, hi)], b[:, 0, :], sin, MULT)
@@ -151,18 +157,22 @@ def tile_attend_freshrope_pl_kernel(tc, emb_words, emb_scales, wk, cosn, sinn, o
         nc.vector.tensor_copy(trig[COS][0][:, span(0, 1)], looked_up(COS, 0, 0, 1))
         gather(COS, 0, 1, 2)
         gather(COS, 0, 2, 4)
-        for n, a in ((SIN, 0), (COS, 1)):
-            for h in range(2):
-                gather(n, a, 2 * h, 2 * h + 2)
+        for lo, hi in ((0, 1), (1, 2), (2, 4)):
+            gather(SIN, 0, lo, hi)
+        for h in range(2):
+            gather(COS, 1, 2 * h, 2 * h + 2)
         for h in (1, 0):
             gather(SIN, 1, 2 * h, 2 * h + 2)
-        for h in range(2):
-            cos_term(0, 2 * h, 2 * h + 2)
-        for lo, hi in ((0, 1), (1, 2), (2, 4)):
-            sin_term(0, lo, hi)
-            add(nc.gpsimd, 0, lo, hi)
-            if hi % 2 == 0:
-                store(0, hi // 2 - 1)
+        cos_term(0, 0, 2)
+        cos_term(0, 2, 3)
+        for q in range(2):
+            sin_term(0, q, q + 1)
+            add(nc.gpsimd, 0, q, q + 1)
+        store(0, 0)
+        cos_term(0, 3, 4)
+        sin_term(0, 2, 4)
+        add(nc.gpsimd, 0, 2, 4)
+        store(0, 1)
         for h in range(2):
             cos_term(1, 2 * h, 2 * h + 2)
         nc.scalar.copy(y_halves[0][:, :, 0:2], ys[:, 0:2, slots(0)].rearrange("p t i -> p i t"))

@@ -20,7 +20,8 @@ COPY = mybir.ActivationFunctionType.Copy
 P = 128
 PACK = 4
 HALF = I // 2
-QUARTER = I // 4
+UNIT = 32
+FIRST = 3
 LIST_COLS = I // 16
 W_SPLIT = 96
 COS, SIN = 0, 1
@@ -62,16 +63,19 @@ def tile_attend_freshrope_pl_kernel(tc, emb_words, emb_scales, wk, cosn, sinn, o
         trig = [[sb.tile([P, I], F32, name="trig%d%d" % (n, a)) for a in range(2)] for n in range(2)]
 
         def span(lo, hi):
-            return slice(lo * QUARTER, hi * QUARTER)
+            return slice(lo * UNIT, hi * UNIT)
+
+        def quarter(q):
+            return span(4 * q, 4 * q + 4)
 
         def looked_up(n, a, lo, hi):
-            return tables[n][a][:].indirect(pos[:, lo * LIST_COLS // 4 : hi * LIST_COLS // 4])
+            return tables[n][a][:].indirect(pos[:, lo * UNIT // 16 : hi * UNIT // 16])
 
         terms = [[sb.tile([P, 2, I], F32, name="term%d%d" % (n, a)) for a in range(2)] for n in range(2)]
 
         def gathered(n, a, lo, hi):
-            if (n, a) == (SIN, 0) and lo < 2:
-                return terms[COS][0][:, lo, span(3, 4)]
+            if (n, a, lo) == (SIN, 0, 0):
+                return terms[COS][0][:, 0, span(12, 12 + FIRST)]
             return trig[n][a][:, span(lo, hi)]
 
         def gather(n, a, lo, hi):
@@ -117,10 +121,10 @@ def tile_attend_freshrope_pl_kernel(tc, emb_words, emb_scales, wk, cosn, sinn, o
         words = out_1[0].rearrange("p n t -> p (n t)").bitcast(I32)
 
         def bank(a, lo, hi):
-            return banks[a][lo // 2][:, :, span(lo % 2, lo % 2 + hi - lo)]
+            return banks[a][lo // 8][:, :, span(lo % 8, lo % 8 + hi - lo)]
 
         def cos_term(a, lo, hi):
-            cos = trig[COS][a][:, span(lo, hi)].unsqueeze(1).to_broadcast([P, 2, (hi - lo) * QUARTER])
+            cos = trig[COS][a][:, span(lo, hi)].unsqueeze(1).to_broadcast([P, 2, (hi - lo) * UNIT])
             nc.vector.tensor_tensor(terms[COS][a][:, :, span(lo, hi)], bank(a, lo, hi), cos, MULT)
 
         def sin_term(a, lo, hi):
@@ -136,57 +140,58 @@ def tile_attend_freshrope_pl_kernel(tc, emb_words, emb_scales, wk, cosn, sinn, o
             nc.sync.dma_start(out_view[:, 2 * a : 2 * a + 2, slots(h)], ys[:, 2 * a : 2 * a + 2, slots(h)])
 
         y_halves = [sb.tile([P, HALF, PACK], BF16, name="y_bf%d" % h, tag=("table11", "y_bf1")[h], align_bytes=64) for h in range(2)]
-        y_bf = [y_halves[q // 2][:, span(q % 2, q % 2 + 1), :] for q in range(4)]
+        y_bf = [y_halves[q // 2][:, quarter(q % 2), :] for q in range(4)]
         y_codes = sb.tile([P, I], U32, name="y_codes", align_bytes=64)
         y_scales = sb.tile([P, I], U8, name="y_scales", align_bytes=64)
 
         def round_y(copy, q):
-            cols = span(q, q + 1)
+            cols = quarter(q)
             copy(y_bf[q].rearrange("p (c i) t -> p c t i", i=4), ys[:, :, cols].rearrange("p t (c i) -> p c t i", i=4))
 
         def round_pair(copy, q, a):
-            copy(y_bf[q][:, :, 2 * a : 2 * a + 2], ys[:, 2 * a : 2 * a + 2, span(q, q + 1)].rearrange("p t i -> p i t"))
+            copy(y_bf[q][:, :, 2 * a : 2 * a + 2], ys[:, 2 * a : 2 * a + 2, quarter(q)].rearrange("p t i -> p i t"))
 
         def quantize(q):
-            cols = span(q, q + 1)
+            cols = quarter(q)
             nc.vector.quantize_mx(out=y_codes[:, cols].bitcast(FP8X4), scales=y_scales[:, cols], in_=y_bf[q].rearrange("p i t -> p (i t)"))
 
         def store_codes(h):
             nc.sync.dma_start(words[:, slots(h)], y_codes[:, slots(h)].bitcast(I32))
 
-        nc.vector.tensor_copy(trig[COS][0][:, span(0, 1)], looked_up(COS, 0, 0, 1))
-        gather(COS, 0, 1, 2)
-        gather(COS, 0, 2, 4)
-        for lo, hi in ((0, 1), (1, 2), (2, 4)):
+        nc.vector.tensor_copy(trig[COS][0][:, quarter(0)], looked_up(COS, 0, 0, 4))
+        gather(COS, 0, 4, 8)
+        gather(COS, 0, 8, 16)
+        pieces = ((0, FIRST), (FIRST, 8), (8, 16))
+        for lo, hi in pieces:
             gather(SIN, 0, lo, hi)
         for h in range(2):
-            gather(COS, 1, 2 * h, 2 * h + 2)
+            gather(COS, 1, 8 * h, 8 * h + 8)
         for h in (1, 0):
-            gather(SIN, 1, 2 * h, 2 * h + 2)
-        cos_term(0, 0, 2)
-        cos_term(0, 2, 3)
-        for q in range(2):
-            sin_term(0, q, q + 1)
-            add(nc.gpsimd, 0, q, q + 1)
+            gather(SIN, 1, 8 * h, 8 * h + 8)
+        cos_term(0, 0, 8)
+        cos_term(0, 8, 12)
+        for lo, hi in pieces[:2]:
+            sin_term(0, lo, hi)
+            add(nc.gpsimd, 0, lo, hi)
         store(0, 0)
-        cos_term(0, 3, 4)
-        sin_term(0, 2, 4)
-        add(nc.gpsimd, 0, 2, 4)
+        cos_term(0, 12, 16)
+        sin_term(0, 8, 16)
+        add(nc.gpsimd, 0, 8, 16)
         store(0, 1)
         for h in range(2):
-            cos_term(1, 2 * h, 2 * h + 2)
+            cos_term(1, 8 * h, 8 * h + 8)
         nc.scalar.copy(y_halves[0][:, :, 0:2], ys[:, 0:2, slots(0)].rearrange("p t i -> p i t"))
-        sin_term(1, 2, 4)
-        sin_term(1, 0, 1)
-        add(nc.vector, 1, 2, 3)
+        sin_term(1, 8, 16)
+        sin_term(1, 0, 4)
+        add(nc.vector, 1, 8, 12)
         round_y(nc.scalar.copy, 2)
-        sin_term(1, 1, 2)
-        add(nc.vector, 1, 3, 4)
+        sin_term(1, 4, 8)
+        add(nc.vector, 1, 12, 16)
         store(1, 1)
         round_y(nc.scalar.copy, 3)
-        add(nc.vector, 1, 0, 1)
+        add(nc.vector, 1, 0, 4)
         round_pair(nc.scalar.copy, 0, 1)
-        add(nc.vector, 1, 1, 2)
+        add(nc.vector, 1, 4, 8)
         store(1, 0)
         quantize(2)
         round_pair(nc.vector.tensor_copy, 1, 1)

@@ -22,6 +22,7 @@ PACK = 4
 HALF = I // 2
 UNIT = 32
 FIRST = 3
+LATE = 4
 LIST_COLS = I // 16
 W_SPLIT = 96
 COS, SIN = 0, 1
@@ -133,27 +134,32 @@ def tile_attend_freshrope_pl_kernel(tc, emb_words, emb_scales, wk, cosn, sinn, o
             nc.vector.scalar_tensor_tensor(terms[SIN][a][:, 0, span(lo, hi)], b[:, 1, :], -1.0, sin, MULT, MULT)
             nc.vector.tensor_tensor(terms[SIN][a][:, 1, span(lo, hi)], b[:, 0, :], sin, MULT)
 
+        def sin_row(e):
+            b = bank(1, 0, 8)
+            if e == 0:
+                nc.vector.scalar_tensor_tensor(terms[SIN][1][:, 0, slots(0)], b[:, 1, :], -1.0, trig[SIN][1][:, slots(0)], MULT, MULT)
+            else:
+                nc.vector.tensor_tensor(terms[SIN][1][:, 1, slots(0)], b[:, 0, :], trig[SIN][1][:, slots(0)], MULT)
+
         def add(engine, a, lo, hi):
             engine.tensor_tensor(ys[:, 2 * a : 2 * a + 2, span(lo, hi)], terms[COS][a][:, :, span(lo, hi)], terms[SIN][a][:, :, span(lo, hi)], ADD)
 
         def store(a, h):
             nc.sync.dma_start(out_view[:, 2 * a : 2 * a + 2, slots(h)], ys[:, 2 * a : 2 * a + 2, slots(h)])
 
-        y_halves = [sb.tile([P, HALF, PACK], BF16, name="y_bf%d" % h, tag=("table11", "y_bf1")[h], align_bytes=64) for h in range(2)]
-        y_bf = [y_halves[q // 2][:, quarter(q % 2), :] for q in range(4)]
+        y_bf = [sb.tile([P, HALF, PACK], BF16, name="y_bf%d" % h, align_bytes=64) for h in range(2)]
         y_codes = sb.tile([P, I], U32, name="y_codes", align_bytes=64)
         y_scales = sb.tile([P, I], U8, name="y_scales", align_bytes=64)
 
-        def round_y(copy, q):
-            cols = quarter(q)
-            copy(y_bf[q].rearrange("p (c i) t -> p c t i", i=4), ys[:, :, cols].rearrange("p t (c i) -> p c t i", i=4))
+        def rounded(lo, hi):
+            return y_bf[lo // 8][:, span(lo % 8, lo % 8 + hi - lo), :]
 
-        def round_pair(copy, q, a):
-            copy(y_bf[q][:, :, 2 * a : 2 * a + 2], ys[:, 2 * a : 2 * a + 2, quarter(q)].rearrange("p t i -> p i t"))
+        def round_y(copy, lo, hi):
+            copy(rounded(lo, hi).rearrange("p (c i) t -> p c t i", i=4), ys[:, :, span(lo, hi)].rearrange("p t (c i) -> p c t i", i=4))
 
-        def quantize(q):
-            cols = quarter(q)
-            nc.vector.quantize_mx(out=y_codes[:, cols].bitcast(FP8X4), scales=y_scales[:, cols], in_=y_bf[q].rearrange("p i t -> p (i t)"))
+        def quantize(lo, hi):
+            cols = span(lo, hi)
+            nc.vector.quantize_mx(out=y_codes[:, cols].bitcast(FP8X4), scales=y_scales[:, cols], in_=rounded(lo, hi).rearrange("p i t -> p (i t)"))
 
         def store_codes(h):
             nc.sync.dma_start(words[:, slots(h)], y_codes[:, slots(h)].bitcast(I32))
@@ -180,25 +186,23 @@ def tile_attend_freshrope_pl_kernel(tc, emb_words, emb_scales, wk, cosn, sinn, o
         store(0, 1)
         for h in range(2):
             cos_term(1, 8 * h, 8 * h + 8)
-        nc.scalar.copy(y_halves[0][:, :, 0:2], ys[:, 0:2, slots(0)].rearrange("p t i -> p i t"))
         sin_term(1, 8, 16)
-        sin_term(1, 0, 4)
+        sin_row(0)
         add(nc.vector, 1, 8, 12)
-        round_y(nc.scalar.copy, 2)
-        sin_term(1, 4, 8)
+        round_y(nc.scalar.copy, 8, 12)
+        sin_row(1)
         add(nc.vector, 1, 12, 16)
         store(1, 1)
-        round_y(nc.scalar.copy, 3)
-        add(nc.vector, 1, 0, 4)
-        round_pair(nc.scalar.copy, 0, 1)
-        add(nc.vector, 1, 4, 8)
+        round_y(nc.scalar.copy, 12, 16)
+        add(nc.vector, 1, 0, 8)
         store(1, 0)
-        quantize(2)
-        round_pair(nc.vector.tensor_copy, 1, 1)
-        quantize(3)
+        round_y(nc.scalar.copy, 0, LATE)
+        quantize(8, 12)
+        round_y(nc.vector.tensor_copy, LATE, 8)
+        quantize(12, 16)
         store_codes(1)
-        quantize(0)
-        quantize(1)
+        quantize(4, 8)
+        quantize(0, 4)
         store_codes(0)
         for q in range(4):
             queue = nc.sync if q < 2 else nc.scalar

@@ -21,7 +21,7 @@ P = 128
 PACK = 4
 HALF = I // 2
 UNIT = 32
-FIRST = 3
+FIRST = 2
 LATE = 4
 LIST_COLS = I // 16
 W_SPLIT = 96

@@ -19,6 +19,7 @@ COPY = mybir.ActivationFunctionType.Copy
 
 P = 128
 PACK = 4
+ALIGN = 256
 HALF = I // 2
 UNIT = 32
 FIRST = 2
@@ -36,10 +37,10 @@ def tile_attend_freshrope_pl_kernel(tc, emb_words, emb_scales, wk, cosn, sinn, o
 
         tok = sb.tile([P, LIST_COLS], U16, name="tok")
         pos = sb.tile([P, LIST_COLS], U16, name="pos")
-        w_raw = sb.tile([P, PACK, D], F32, name="w_raw")
-        e_pool = sb.tile([P, T], I32, name="e_pool", align_bytes=64)
-        s_pool = sb.tile([P, T], U8, name="s_pool", align_bytes=64)
-        tables = [[sb.tile([P, U], F32, name="table%d%d" % (n, a), tag="table%d%d" % (n, a), align_bytes=64) for a in range(2)] for n in range(2)]
+        w_raw = sb.tile([P, PACK, D], F32, name="w_raw", align_bytes=ALIGN)
+        e_pool = sb.tile([P, T], I32, name="e_pool", align_bytes=ALIGN)
+        s_pool = sb.tile([P, T], U8, name="s_pool", align_bytes=ALIGN)
+        tables = [[sb.tile([P, U], F32, name="table%d%d" % (n, a), tag="table%d%d" % (n, a), align_bytes=ALIGN) for a in range(2)] for n in range(2)]
 
         def load_table(n, a):
             nc.sync.dma_start(tables[n][a][:], (cosn, sinn)[n].rearrange("(p t) u -> p t u", t=PACK)[:, 2 * a, :])
@@ -61,7 +62,7 @@ def tile_attend_freshrope_pl_kernel(tc, emb_words, emb_scales, wk, cosn, sinn, o
         def entries(lst, h):
             return lst[:, h * LIST_COLS // 2 : (h + 1) * LIST_COLS // 2]
 
-        trig = [[sb.tile([P, I], F32, name="trig%d%d" % (n, a)) for a in range(2)] for n in range(2)]
+        trig = [[sb.tile([P, I], F32, name="trig%d%d" % (n, a), align_bytes=ALIGN) for a in range(2)] for n in range(2)]
 
         def span(lo, hi):
             return slice(lo * UNIT, hi * UNIT)
@@ -72,7 +73,7 @@ def tile_attend_freshrope_pl_kernel(tc, emb_words, emb_scales, wk, cosn, sinn, o
         def looked_up(n, a, lo, hi):
             return tables[n][a][:].indirect(pos[:, lo * UNIT // 16 : hi * UNIT // 16])
 
-        terms = [[sb.tile([P, 2, I], F32, name="term%d%d" % (n, a)) for a in range(2)] for n in range(2)]
+        terms = [[sb.tile([P, 2, I], F32, name="term%d%d" % (n, a), align_bytes=ALIGN) for a in range(2)] for n in range(2)]
 
         def gathered(n, a, lo, hi):
             if (n, a, lo) == (SIN, 0, 0):
@@ -82,10 +83,10 @@ def tile_attend_freshrope_pl_kernel(tc, emb_words, emb_scales, wk, cosn, sinn, o
         def gather(n, a, lo, hi):
             nc.scalar.activation(gathered(n, a, lo, hi), looked_up(n, a, lo, hi), COPY)
 
-        w_codes = sb.tile([P, D], U32, name="w_codes", align_bytes=64)
-        w_scales = sb.tile([P, D], U8, name="w_scales", align_bytes=64)
+        w_codes = sb.tile([P, D], U32, name="w_codes", align_bytes=ALIGN)
+        w_scales = sb.tile([P, D], U8, name="w_scales", align_bytes=ALIGN)
         w_view = w_raw[:].rearrange("p j (m t) -> p m t j", t=PACK)
-        w_bf = [sb.tile([P, 2, P, PACK], BF16, name="w_bf%d" % a, tag="w_bf%d" % a, align_bytes=64) for a in range(2)]
+        w_bf = [sb.tile([P, 2, P, PACK], BF16, name="w_bf%d" % a, tag="w_bf%d" % a, align_bytes=ALIGN) for a in range(2)]
 
         def round_w(copy, a, lo, hi):
             copy(w_bf[a][:, :, lo:hi, :].rearrange("p t m j -> p m t j"), w_view[:, lo:hi, 2 * a : 2 * a + 2, :])
@@ -97,9 +98,9 @@ def tile_attend_freshrope_pl_kernel(tc, emb_words, emb_scales, wk, cosn, sinn, o
             cols = slice(2 * P * a, 2 * P * (a + 1))
             nc.vector.quantize_mx(out=w_codes[:, cols].bitcast(FP8X4), scales=w_scales[:, cols], in_=w_bf[a][:].rearrange("p t m j -> p (t m j)"))
 
-        e_scales = sb.tile([P, I], U8, name="e_scales", tag="w_bf1", align_bytes=64)
+        e_scales = sb.tile([P, I], U8, name="e_scales", tag="w_bf1", align_bytes=ALIGN)
         nc.vector.tensor_copy(e_scales[:], s_pool[:].indirect(tok[:]))
-        e_codes = sb.tile([P, I], U32, name="e_codes", align_bytes=64)
+        e_codes = sb.tile([P, I], U32, name="e_codes", align_bytes=ALIGN)
         banks = [[ps.tile([P, 2, HALF], F32, name="bank%d%d" % (a, h)) for h in range(2)] for a in range(2)]
         for h in range(2):
             nc.vector.tensor_copy(e_codes[:, slots(h)], e_pool[:].bitcast(U32).indirect(entries(tok, h)))
@@ -117,7 +118,7 @@ def tile_attend_freshrope_pl_kernel(tc, emb_words, emb_scales, wk, cosn, sinn, o
                         stop=True,
                     )
 
-        ys = sb.tile([P, PACK, I], F32, name="ys")
+        ys = sb.tile([P, PACK, I], F32, name="ys", align_bytes=ALIGN)
         out_view = out_0.rearrange("(p t) i -> p t i", t=PACK)
         words = out_1[0].rearrange("p n t -> p (n t)").bitcast(I32)
 
@@ -147,9 +148,9 @@ def tile_attend_freshrope_pl_kernel(tc, emb_words, emb_scales, wk, cosn, sinn, o
         def store(a, h):
             nc.sync.dma_start(out_view[:, 2 * a : 2 * a + 2, slots(h)], ys[:, 2 * a : 2 * a + 2, slots(h)])
 
-        y_bf = [sb.tile([P, HALF, PACK], BF16, name="y_bf%d" % h, align_bytes=64) for h in range(2)]
-        y_codes = sb.tile([P, I], U32, name="y_codes", align_bytes=64)
-        y_scales = sb.tile([P, I], U8, name="y_scales", align_bytes=64)
+        y_bf = [sb.tile([P, HALF, PACK], BF16, name="y_bf%d" % h, align_bytes=ALIGN) for h in range(2)]
+        y_codes = sb.tile([P, I], U32, name="y_codes", align_bytes=ALIGN)
+        y_scales = sb.tile([P, I], U8, name="y_scales", align_bytes=ALIGN)
 
         def rounded(lo, hi):
             return y_bf[lo // 8][:, span(lo % 8, lo % 8 + hi - lo), :]

@@ -78,6 +78,8 @@ def tile_attend_freshrope_pl_kernel(tc, emb_words, emb_scales, wk, cosn, sinn, o
         def gathered(n, a, lo, hi):
             if (n, a, lo) == (SIN, 0, 0):
                 return terms[COS][0][:, 0, span(12, 12 + FIRST)]
+            if (n, a) == (COS, 1):
+                return trig[n][a][:, slots(0)]
             return trig[n][a][:, span(lo, hi)]
 
         def gather(n, a, lo, hi):
@@ -98,7 +100,7 @@ def tile_attend_freshrope_pl_kernel(tc, emb_words, emb_scales, wk, cosn, sinn, o
             cols = slice(2 * P * a, 2 * P * (a + 1))
             nc.vector.quantize_mx(out=w_codes[:, cols].bitcast(FP8X4), scales=w_scales[:, cols], in_=w_bf[a][:].rearrange("p t m j -> p (t m j)"))
 
-        e_scales = sb.tile([P, I], U8, name="e_scales", tag="w_bf1", align_bytes=ALIGN)
+        e_scales = sb.tile([P, I], U8, name="e_scales", align_bytes=ALIGN)
         nc.vector.tensor_copy(e_scales[:], s_pool[:].indirect(tok[:]))
         e_codes = sb.tile([P, I], U32, name="e_codes", align_bytes=ALIGN)
         banks = [[ps.tile([P, 2, HALF], F32, name="bank%d%d" % (a, h)) for h in range(2)] for a in range(2)]
@@ -126,7 +128,7 @@ def tile_attend_freshrope_pl_kernel(tc, emb_words, emb_scales, wk, cosn, sinn, o
             return banks[a][lo // 8][:, :, span(lo % 8, lo % 8 + hi - lo)]
 
         def cos_term(a, lo, hi):
-            cos = trig[COS][a][:, span(lo, hi)].unsqueeze(1).to_broadcast([P, 2, (hi - lo) * UNIT])
+            cos = gathered(COS, a, lo, hi).unsqueeze(1).to_broadcast([P, 2, (hi - lo) * UNIT])
             nc.vector.tensor_tensor(terms[COS][a][:, :, span(lo, hi)], bank(a, lo, hi), cos, MULT)
 
         def sin_term(a, lo, hi):
@@ -134,13 +136,6 @@ def tile_attend_freshrope_pl_kernel(tc, emb_words, emb_scales, wk, cosn, sinn, o
             b = bank(a, lo, hi)
             nc.vector.scalar_tensor_tensor(terms[SIN][a][:, 0, span(lo, hi)], b[:, 1, :], -1.0, sin, MULT, MULT)
             nc.vector.tensor_tensor(terms[SIN][a][:, 1, span(lo, hi)], b[:, 0, :], sin, MULT)
-
-        def sin_row(e):
-            b = bank(1, 0, 8)
-            if e == 0:
-                nc.vector.scalar_tensor_tensor(terms[SIN][1][:, 0, slots(0)], b[:, 1, :], -1.0, trig[SIN][1][:, slots(0)], MULT, MULT)
-            else:
-                nc.vector.tensor_tensor(terms[SIN][1][:, 1, slots(0)], b[:, 0, :], trig[SIN][1][:, slots(0)], MULT)
 
         def add(engine, a, lo, hi):
             engine.tensor_tensor(ys[:, 2 * a : 2 * a + 2, span(lo, hi)], terms[COS][a][:, :, span(lo, hi)], terms[SIN][a][:, :, span(lo, hi)], ADD)
@@ -171,8 +166,7 @@ def tile_attend_freshrope_pl_kernel(tc, emb_words, emb_scales, wk, cosn, sinn, o
         pieces = ((0, FIRST), (FIRST, 8), (8, 16))
         for lo, hi in pieces:
             gather(SIN, 0, lo, hi)
-        for h in range(2):
-            gather(COS, 1, 8 * h, 8 * h + 8)
+        gather(COS, 1, 8, 16)
         for h in (1, 0):
             gather(SIN, 1, 8 * h, 8 * h + 8)
         cos_term(0, 0, 8)
@@ -185,13 +179,13 @@ def tile_attend_freshrope_pl_kernel(tc, emb_words, emb_scales, wk, cosn, sinn, o
         sin_term(0, 8, 16)
         add(nc.gpsimd, 0, 8, 16)
         store(0, 1)
-        for h in range(2):
-            cos_term(1, 8 * h, 8 * h + 8)
+        cos_term(1, 8, 16)
+        gather(COS, 1, 0, 8)
         sin_term(1, 8, 16)
-        sin_row(0)
-        add(nc.vector, 1, 8, 12)
+        add(nc.gpsimd, 1, 8, 12)
         round_y(nc.scalar.copy, 8, 12)
-        sin_row(1)
+        sin_term(1, 0, 8)
+        cos_term(1, 0, 8)
         add(nc.vector, 1, 12, 16)
         store(1, 1)
         round_y(nc.scalar.copy, 12, 16)

@@ -24,6 +24,7 @@ HALF = I // 2
 UNIT = 32
 FIRST = 2
 LATE = 4
+DEFER = 4
 LIST_COLS = I // 16
 W_SPLIT = 96
 COS, SIN = 0, 1
@@ -78,8 +79,8 @@ def tile_attend_freshrope_pl_kernel(tc, emb_words, emb_scales, wk, cosn, sinn, o
         def gathered(n, a, lo, hi):
             if (n, a, lo) == (SIN, 0, 0):
                 return terms[COS][0][:, 0, span(12, 12 + FIRST)]
-            if (n, a) == (COS, 1):
-                return trig[n][a][:, slots(0)]
+            if (n, a, lo) == (COS, 1, 0):
+                return trig[n][a][:, span(8, 8 + hi)]
             return trig[n][a][:, span(lo, hi)]
 
         def gather(n, a, lo, hi):
@@ -167,6 +168,7 @@ def tile_attend_freshrope_pl_kernel(tc, emb_words, emb_scales, wk, cosn, sinn, o
         for lo, hi in pieces:
             gather(SIN, 0, lo, hi)
         gather(COS, 1, 8, 16)
+        gather(COS, 1, DEFER, 8)
         for h in (1, 0):
             gather(SIN, 1, 8 * h, 8 * h + 8)
         cos_term(0, 0, 8)
@@ -180,12 +182,13 @@ def tile_attend_freshrope_pl_kernel(tc, emb_words, emb_scales, wk, cosn, sinn, o
         add(nc.gpsimd, 0, 8, 16)
         store(0, 1)
         cos_term(1, 8, 16)
-        gather(COS, 1, 0, 8)
+        gather(COS, 1, 0, DEFER)
+        cos_term(1, DEFER, 8)
         sin_term(1, 8, 16)
         add(nc.gpsimd, 1, 8, 12)
         round_y(nc.scalar.copy, 8, 12)
         sin_term(1, 0, 8)
-        cos_term(1, 0, 8)
+        cos_term(1, 0, DEFER)
         add(nc.vector, 1, 12, 16)
         store(1, 1)
         round_y(nc.scalar.copy, 12, 16)

@@ -23,7 +23,7 @@ ALIGN = 256
 HALF = I // 2
 UNIT = 32
 FIRST = 2
-LATE = 4
+LATE = 3
 DEFER = 4
 LIST_COLS = I // 16
 W_SPLIT = 96

@@ -49,10 +49,10 @@ def tile_attend_freshrope_pl_kernel(tc, emb_words, emb_scales, wk, cosn, sinn, o
         nc.vector.memset(s_pool[:].bitcast(I32), 0)
         nc.sync.dma_start(w_raw[:], wk.rearrange("(p j) d -> p j d", j=PACK))
         nc.sync.dma_start(tok[:], offs)
-        nc.sync.dma_start(pos[:], offs2)
         for r in range(4):
             nc.sync.dma_start(s_pool[r:P:32, :].bitcast(I32), emb_scales[0].rearrange("(q r) n -> r q n", r=4)[r].bitcast(I32))
         nc.sync.dma_start(e_pool[:], emb_words[0].rearrange("p n t -> p (n t)").bitcast(I32))
+        nc.sync.dma_start(pos[:], offs2)
         for a in range(2):
             for n in (COS, SIN):
                 load_table(n, a)
@@ -88,11 +88,11 @@ def tile_attend_freshrope_pl_kernel(tc, emb_words, emb_scales, wk, cosn, sinn, o
 
         w_codes = sb.tile([P, D], U32, name="w_codes", align_bytes=ALIGN)
         w_scales = sb.tile([P, D], U8, name="w_scales", align_bytes=ALIGN)
-        w_view = w_raw[:].rearrange("p j (m t) -> p m t j", t=PACK)
+        w_view = w_raw[:].rearrange("p j (m t) -> p m j t", t=PACK)
         w_bf = [sb.tile([P, 2, P, PACK], BF16, name="w_bf%d" % a, tag="w_bf%d" % a, align_bytes=ALIGN) for a in range(2)]
 
         def round_w(copy, a, lo, hi):
-            copy(w_bf[a][:, :, lo:hi, :].rearrange("p t m j -> p m t j"), w_view[:, lo:hi, 2 * a : 2 * a + 2, :])
+            copy(w_bf[a][:, :, lo:hi, :].rearrange("p t m j -> p m j t"), w_view[:, lo:hi, :, 2 * a : 2 * a + 2])
 
         round_w(nc.scalar.copy, 1, 0, W_SPLIT)
         round_w(nc.vector.tensor_copy, 0, 0, P)

@@ -24,7 +24,7 @@ HALF = I // 2
 UNIT = 32
 FIRST = 2
 LATE = 3
-DEFER = 4
+DEFER = 6
 LIST_COLS = I // 16
 W_SPLIT = 96
 COS, SIN = 0, 1
@@ -167,8 +167,7 @@ def tile_attend_freshrope_pl_kernel(tc, emb_words, emb_scales, wk, cosn, sinn, o
         pieces = ((0, FIRST), (FIRST, 8), (8, 16))
         for lo, hi in pieces:
             gather(SIN, 0, lo, hi)
-        gather(COS, 1, 8, 16)
-        gather(COS, 1, DEFER, 8)
+        gather(COS, 1, DEFER, 16)
         for h in (1, 0):
             gather(SIN, 1, 8 * h, 8 * h + 8)
         cos_term(0, 0, 8)

@@ -44,7 +44,7 @@ def tile_attend_freshrope_pl_kernel(tc, emb_words, emb_scales, wk, cosn, sinn, o
         tables = [[sb.tile([P, U], F32, name="table%d%d" % (n, a), tag="table%d%d" % (n, a), align_bytes=ALIGN) for a in range(2)] for n in range(2)]
 
         def load_table(n, a):
-            nc.sync.dma_start(tables[n][a][:], (cosn, sinn)[n].rearrange("(p t) u -> p t u", t=PACK)[:, 2 * a, :])
+            nc.sync.dma_start(tables[n][a][:], (cosn, sinn)[n].rearrange("(q r) u -> q r u", r=2 * PACK)[:, 2 * a : 2 * a + PACK + 2 : PACK + 1, :])
 
         nc.vector.memset(s_pool[:].bitcast(I32), 0)
         nc.sync.dma_start(w_raw[:], wk.rearrange("(p j) d -> p j d", j=PACK))

from contextlib import ExitStack

import concourse.mybir as mybir

K, T, I, D, U = 512, 2048, 512, 512, 1024
FLOPS = 2 * K * D * I
BYTES = 128 * T * 4 + 16 * T + K * D * 4 + 2 * (D // 2) * U * 4 + 2 * 128 * 32 * 2 + D * I * 4 + D * I + 16 * I

F32 = mybir.dt.float32
BF16 = mybir.dt.bfloat16
I32 = mybir.dt.int32
U32 = mybir.dt.uint32
U16 = mybir.dt.uint16
U8 = mybir.dt.uint8
FP8X4 = mybir.dt.float8_e4m3fn_x4
MULT = mybir.AluOpType.mult
ADD = mybir.AluOpType.add
COPY = mybir.ActivationFunctionType.Copy

P = 128
PACK = 4
ALIGN = 256
HALF = I // 2
UNIT = 32
FIRST = 2
LATE = 3
DEFER = 6
LIST_COLS = I // 16
W_SPLIT = 96
COS, SIN = 0, 1


def tile_attend_freshrope_pl_kernel(tc, emb_words, emb_scales, wk, cosn, sinn, offs, offs2, out_0, out_1, out_2):
    nc = tc.nc
    with ExitStack() as ctx:
        sb = ctx.enter_context(tc.tile_pool(name="sb", bufs=1))
        ps = ctx.enter_context(tc.psum_pool(name="ps", bufs=1))

        tok = sb.tile([P, LIST_COLS], U16, name="tok")
        pos = sb.tile([P, LIST_COLS], U16, name="pos")
        w_raw = sb.tile([P, PACK, D], F32, name="w_raw", align_bytes=ALIGN)
        e_pool = sb.tile([P, T], I32, name="e_pool", align_bytes=ALIGN)
        s_pool = sb.tile([P, T], U8, name="s_pool", align_bytes=ALIGN)
        tables = [[sb.tile([P, U], F32, name="table%d%d" % (n, a), tag="table%d%d" % (n, a), align_bytes=ALIGN) for a in range(2)] for n in range(2)]

        def load_table(n, a):
            nc.sync.dma_start(tables[n][a][:], (cosn, sinn)[n].rearrange("(q r) u -> q r u", r=2 * PACK)[:, 2 * a : 2 * a + PACK + 2 : PACK + 1, :])

        nc.vector.memset(s_pool[:].bitcast(I32), 0)
        nc.sync.dma_start(w_raw[:], wk.rearrange("(p j) d -> p j d", j=PACK))
        nc.sync.dma_start(tok[:], offs)
        for r in range(4):
            nc.sync.dma_start(s_pool[r:P:32, :].bitcast(I32), emb_scales[0].rearrange("(q r) n -> r q n", r=4)[r].bitcast(I32))
        nc.sync.dma_start(e_pool[:], emb_words[0].rearrange("p n t -> p (n t)").bitcast(I32))
        nc.sync.dma_start(pos[:], offs2)
        for a in range(2):
            for n in (COS, SIN):
                load_table(n, a)

        def slots(h):
            return slice(h * HALF, (h + 1) * HALF)

        def entries(lst, h):
            return lst[:, h * LIST_COLS // 2 : (h + 1) * LIST_COLS // 2]

        trig = [[sb.tile([P, I], F32, name="trig%d%d" % (n, a), align_bytes=ALIGN) for a in range(2)] for n in range(2)]

        def span(lo, hi):
            return slice(lo * UNIT, hi * UNIT)

        def quarter(q):
            return span(4 * q, 4 * q + 4)

        def looked_up(n, a, lo, hi):
            return tables[n][a][:].indirect(pos[:, lo * UNIT // 16 : hi * UNIT // 16])

        terms = [[sb.tile([P, 2, I], F32, name="term%d%d" % (n, a), align_bytes=ALIGN) for a in range(2)] for n in range(2)]

        def gathered(n, a, lo, hi):
            if (n, a, lo) == (SIN, 0, 0):
                return terms[COS][0][:, 0, span(12, 12 + FIRST)]
            if (n, a, lo) == (COS, 1, 0):
                return trig[n][a][:, span(8, 8 + hi)]
            return trig[n][a][:, span(lo, hi)]

        def gather(n, a, lo, hi):
            nc.scalar.activation(gathered(n, a, lo, hi), looked_up(n, a, lo, hi), COPY)

        w_codes = sb.tile([P, D], U32, name="w_codes", align_bytes=ALIGN)
        w_scales = sb.tile([P, D], U8, name="w_scales", align_bytes=ALIGN)
        w_view = w_raw[:].rearrange("p j (m t) -> p m j t", t=PACK)
        w_bf = [sb.tile([P, 2, P, PACK], BF16, name="w_bf%d" % a, tag="w_bf%d" % a, align_bytes=ALIGN) for a in range(2)]

        def round_w(copy, a, lo, hi):
            copy(w_bf[a][:, :, lo:hi, :].rearrange("p t m j -> p m j t"), w_view[:, lo:hi, :, 2 * a : 2 * a + 2])

        round_w(nc.scalar.copy, 1, 0, W_SPLIT)
        round_w(nc.vector.tensor_copy, 0, 0, P)
        round_w(nc.vector.tensor_copy, 1, W_SPLIT, P)
        for a in range(2):
            cols = slice(2 * P * a, 2 * P * (a + 1))
            nc.vector.quantize_mx(out=w_codes[:, cols].bitcast(FP8X4), scales=w_scales[:, cols], in_=w_bf[a][:].rearrange("p t m j -> p (t m j)"))

        e_scales = sb.tile([P, I], U8, name="e_scales", align_bytes=ALIGN)
        nc.vector.tensor_copy(e_scales[:], s_pool[:].indirect(tok[:]))
        e_codes = sb.tile([P, I], U32, name="e_codes", align_bytes=ALIGN)
        banks = [[ps.tile([P, 2, HALF], F32, name="bank%d%d" % (a, h)) for h in range(2)] for a in range(2)]
        for h in range(2):
            nc.vector.tensor_copy(e_codes[:, slots(h)], e_pool[:].bitcast(U32).indirect(entries(tok, h)))
        for a in range(2):
            for h in range(2):
                for e in range(2):
                    cols = slice((2 * a + e) * P, (2 * a + e + 1) * P)
                    nc.tensor.matmul_mx(
                        out=banks[a][h][:, e, :],
                        lhsT=w_codes[:, cols].bitcast(FP8X4),
                        lhsT_scale=w_scales[:, cols],
                        rhs=e_codes[:, slots(h)].bitcast(FP8X4),
                        rhs_scale=e_scales[:, slots(h)],
                        start=True,
                        stop=True,
                    )

        ys = sb.tile([P, PACK, I], F32, name="ys", align_bytes=ALIGN)
        out_view = out_0.rearrange("(p t) i -> p t i", t=PACK)
        words = out_1[0].rearrange("p n t -> p (n t)").bitcast(I32)

        def bank(a, lo, hi):
            return banks[a][lo // 8][:, :, span(lo % 8, lo % 8 + hi - lo)]

        def cos_term(a, lo, hi):
            cos = gathered(COS, a, lo, hi).unsqueeze(1).to_broadcast([P, 2, (hi - lo) * UNIT])
            nc.vector.tensor_tensor(terms[COS][a][:, :, span(lo, hi)], bank(a, lo, hi), cos, MULT)

        def sin_term(a, lo, hi):
            sin = gathered(SIN, a, lo, hi)
            b = bank(a, lo, hi)
            nc.vector.scalar_tensor_tensor(terms[SIN][a][:, 0, span(lo, hi)], b[:, 1, :], -1.0, sin, MULT, MULT)
            nc.vector.tensor_tensor(terms[SIN][a][:, 1, span(lo, hi)], b[:, 0, :], sin, MULT)

        def add(engine, a, lo, hi):
            engine.tensor_tensor(ys[:, 2 * a : 2 * a + 2, span(lo, hi)], terms[COS][a][:, :, span(lo, hi)], terms[SIN][a][:, :, span(lo, hi)], ADD)

        def store(a, h):
            nc.sync.dma_start(out_view[:, 2 * a : 2 * a + 2, slots(h)], ys[:, 2 * a : 2 * a + 2, slots(h)])

        y_bf = [sb.tile([P, HALF, PACK], BF16, name="y_bf%d" % h, align_bytes=ALIGN) for h in range(2)]
        y_codes = sb.tile([P, I], U32, name="y_codes", align_bytes=ALIGN)
        y_scales = sb.tile([P, I], U8, name="y_scales", align_bytes=ALIGN)

        def rounded(lo, hi):
            return y_bf[lo // 8][:, span(lo % 8, lo % 8 + hi - lo), :]

        def round_y(copy, lo, hi):
            copy(rounded(lo, hi).rearrange("p (c i) t -> p c t i", i=4), ys[:, :, span(lo, hi)].rearrange("p t (c i) -> p c t i", i=4))

        def quantize(lo, hi):
            cols = span(lo, hi)
            nc.vector.quantize_mx(out=y_codes[:, cols].bitcast(FP8X4), scales=y_scales[:, cols], in_=rounded(lo, hi).rearrange("p i t -> p (i t)"))

        def store_codes(h):
            nc.sync.dma_start(words[:, slots(h)], y_codes[:, slots(h)].bitcast(I32))

        nc.vector.tensor_copy(trig[COS][0][:, quarter(0)], looked_up(COS, 0, 0, 4))
        gather(COS, 0, 4, 8)
        gather(COS, 0, 8, 16)
        pieces = ((0, FIRST), (FIRST, 8), (8, 16))
        for lo, hi in pieces:
            gather(SIN, 0, lo, hi)
        gather(COS, 1, DEFER, 16)
        for h in (1, 0):
            gather(SIN, 1, 8 * h, 8 * h + 8)
        cos_term(0, 0, 8)
        cos_term(0, 8, 12)
        for lo, hi in pieces[:2]:
            sin_term(0, lo, hi)
            add(nc.gpsimd, 0, lo, hi)
        store(0, 0)
        cos_term(0, 12, 16)
        sin_term(0, 8, 16)
        add(nc.gpsimd, 0, 8, 16)
        store(0, 1)
        cos_term(1, 8, 16)
        gather(COS, 1, 0, DEFER)
        cos_term(1, DEFER, 8)
        sin_term(1, 8, 16)
        add(nc.gpsimd, 1, 8, 12)
        round_y(nc.scalar.copy, 8, 12)
        sin_term(1, 0, 8)
        cos_term(1, 0, DEFER)
        add(nc.vector, 1, 12, 16)
        store(1, 1)
        round_y(nc.scalar.copy, 12, 16)
        add(nc.vector, 1, 0, 8)
        store(1, 0)
        round_y(nc.scalar.copy, 0, LATE)
        quantize(8, 12)
        round_y(nc.vector.tensor_copy, LATE, 8)
        quantize(12, 16)
        store_codes(1)
        quantize(4, 8)
        quantize(0, 4)
        store_codes(0)
        for q in range(4):
            queue = nc.sync if q < 2 else nc.scalar
            queue.dma_start(out_2[0, 4 * q : 4 * q + 4, :].bitcast(I32), y_scales[32 * q : 32 * q + 4, :].bitcast(I32))
